import numpy as np
import ml_dtypes


def mxq(x, axis, fmt="e4m3"):
    dtype, down = {"e4m3": (ml_dtypes.float8_e4m3fn, 7), "e5m2": (ml_dtypes.float8_e5m2, 14)}[fmt]
    v = np.moveaxis(np.asarray(x, np.float32).astype(ml_dtypes.bfloat16).astype(np.float64), axis, -1)
    blocks = v.reshape(v.shape[:-1] + (-1, 32))
    amax = np.abs(blocks).max(-1, keepdims=True)
    byte = np.maximum(np.where(amax > 0, np.frexp(amax)[1] - 1 + 127, 0) - down, 1)
    scale = np.exp2(byte - 127.0)
    codes = (blocks / scale).astype(np.float32).astype(dtype).astype(np.float64)
    return np.moveaxis((codes * scale).reshape(v.shape), -1, axis)


WIDE = False


def mx_kscale(k):
    if not WIDE:
        return np.ones(k)
    levels = np.array([10, -10, 5, -5, 0])
    if k % 512:
        return np.exp2(np.random.permutation(np.resize(levels, k // 32))).repeat(32)
    a = np.empty((k // 512, 16))
    for p in range(k // 512):
        a[p, :8] = np.random.permutation(np.resize(levels, 8))
        for g in range(8):
            far = levels[np.abs(levels - a[p, g]) >= 10]
            a[p, g + 8] = far[np.random.randint(len(far))]
    return np.exp2(a.ravel()).repeat(32)


def f64(x):
    return np.asarray(x).astype(np.float64)


def striped(idx):
    return np.tile(idx.reshape(-1, 16).T, (8, 1)).astype(np.uint16)


def unstriped(offs):
    return offs[:16].T.reshape(-1).astype(np.int64)


E2M1 = np.array([0.0, 0.5, 1.0, 1.5, 2.0, 3.0, 4.0, 6.0, -0.0, -0.5, -1.0, -1.5, -2.0, -3.0, -4.0, -6.0])


def pack_weight(w, fmt):
    k, n = w.shape
    w = f64(np.asarray(w, np.float32).astype(ml_dtypes.bfloat16)).reshape(k // 32, 32, n)
    amax = np.abs(w).max(1)
    if fmt == "e4m3":
        byte = np.frexp(amax)[1] - 1 + 127 - 7
    else:
        mant, ex = np.frexp(amax / 6.0)
        byte = np.where(mant > 0.5, ex, ex - 1) + 127
    byte = np.clip(np.where(amax > 0, byte, 1), 1, 254)
    scaled = (w * np.exp2(127.0 - byte)[:, None, :]).reshape(k, n).astype(np.float32)
    by_word = np.ascontiguousarray(scaled.reshape(k // 512, 128, 4, n).transpose(0, 1, 3, 2))
    if fmt == "e4m3":
        words = by_word.astype(ml_dtypes.float8_e4m3fn).view(np.uint8)
    else:
        c = by_word.astype(ml_dtypes.float4_e2m1fn).view(np.uint8) & 0xF
        words = (c[..., 0::2] | (c[..., 1::2] << 4)).reshape(k // 512, 128, 2 * n)
    return np.ascontiguousarray(words), np.ascontiguousarray(byte.astype(np.uint8).reshape(k // 512, 16, n))


def unpack_weight(words, scales, fmt):
    g, _, n = scales.shape
    words = np.ascontiguousarray(words).reshape(g, 128, n, -1)
    if fmt == "e4m3":
        vals = words.view(ml_dtypes.float8_e4m3fn).astype(np.float64)
    else:
        nib = np.empty((g, 128, n, 4), np.uint8)
        nib[..., 0::2] = words & 0xF
        nib[..., 1::2] = words >> 4
        vals = E2M1[nib]
    vals = vals * np.repeat(np.exp2(scales.astype(np.float64) - 127.0), 8, axis=1)[..., None]
    return vals.transpose(0, 1, 3, 2).reshape(g * 512, n)


def gelu(v):
    return 0.5 * v * (1.0 + np.tanh(np.sqrt(2.0 / np.pi) * (v + 0.044715 * v**3)))


K, H, T, S, P = 1536, 1024, 4096, 1024, 512

def setup_inputs():
    n = np.random.standard_normal
    s = mx_kscale(K)[:, None]
    u = mx_kscale(H)[:, None]
    tab_words, tab_scales = pack_weight(n((K, T)) * s, "e4m3")
    wp_words, wp_scales = pack_weight(n((H, H)) / np.sqrt(H) / u, "e2m1")
    return {
        "tab_words": tab_words, "tab_scales": tab_scales,
        "offs": striped(np.random.permutation(T)[:S]),
        "pos1": striped(np.random.permutation(S)[:P]),
        "pos2": striped(np.random.permutation(S)[:P]),
        "w1": (n((K, H)) / np.sqrt(K) / s * u.T).astype(np.float32),
        "b1": (0.3 * n(H) * u[:, 0]).astype(np.float32),
        "wp_words": wp_words, "wp_scales": wp_scales,
        "gd": (np.exp(0.3 * n(H)) / u[:, 0]).astype(np.float32),
    }

def reference(tab_words, tab_scales, offs, pos1, pos2, w1, b1, wp_words, wp_scales, gd):
    v = unpack_weight(tab_words, tab_scales, "e4m3")[:, unstriped(offs)]
    h = (mxq(f64(w1), 0, "e4m3").T @ v) + f64(b1)[:, None]
    x = np.abs(h[:, unstriped(pos1)])
    wp = unpack_weight(wp_words, wp_scales, "e2m1")
    y = wp.T @ mxq(x, 0, "e4m3")
    d = f64(gd)[:, None] * h[:, unstriped(pos2)]
    out = d / (1.0 + np.abs(y))
    return out

@@ -1,0 +1,303 @@
+from contextlib import ExitStack
+
+import concourse.mybir as mybir
+
+K, H, T, S, M = 1536, 1024, 4096, 1024, 512
+FLOPS = 2 * K * H * S + 2 * H * H * M
+
+F32 = mybir.dt.float32
+BF16 = mybir.dt.bfloat16
+I32 = mybir.dt.int32
+U32 = mybir.dt.uint32
+U16 = mybir.dt.uint16
+U8 = mybir.dt.uint8
+FP8X4 = mybir.dt.float8_e4m3fn_x4
+FP4X4 = mybir.dt.float4_e2m1fn_x4
+ACT = mybir.ActivationFunctionType
+MULT = mybir.AluOpType.mult
+ADD = mybir.AluOpType.add
+
+P = 128
+PACK = 4
+KP = P * PACK
+BANK = 512
+PASSES = K // KP
+BLOCKS = H // KP
+HALVES = S // BANK
+SCALAR_SHARE = 40
+LAST_SHARE = 128
+SQUARES_ON_SCALAR = 6
+
+
+def tile_list_cocoa_supply_tiers_kernel(
+    tc, tab_words, tab_scales, offs, pos1, pos2, w1, b1, wp_words, wp_scales, gd, out
+):
+    nc = tc.nc
+    with ExitStack() as ctx:
+        lists = ctx.enter_context(tc.tile_pool(name="lists", bufs=1))
+        keep = ctx.enter_context(tc.tile_pool(name="keep", bufs=1))
+        ring = ctx.enter_context(tc.tile_pool(name="ring", bufs=3))
+        psum = ctx.enter_context(tc.psum_pool(name="psum", bufs=1))
+
+        offs_sb = lists.tile([P, S // 16], U16, name="offs_sb")
+        pos1_sb = lists.tile([P, M // 16], U16, name="pos1_sb")
+        pos2_sb = lists.tile([P, M // 16], U16, name="pos2_sb")
+
+        tab_sc = keep.tile([P, T], U8, name="tab_sc", align_bytes=64)
+        wp_sc_raw = keep.tile([P, BLOCKS * H], U8, name="wp_sc_raw", align_bytes=64)
+        nc.vector.memset(tab_sc[:].bitcast(I32), 0)
+        nc.vector.memset(wp_sc_raw[:].bitcast(I32), 0)
+        warm = keep.tile([P, 8], F32, name="warm")
+        nc.vector.memset(warm[:, 0:1], 1.0)
+        nc.scalar.activation(warm[:, 1:2], warm[:, 0:1], ACT.Abs_reciprocal_sqrt)
+        b1_sb = keep.tile([P, BLOCKS, PACK], F32, name="b1_sb")
+        gd_sb = keep.tile([P, BLOCKS, PACK], F32, name="gd_sb")
+
+        tab_w = [keep.tile([P, T], U32, name=f"tab_w{a}") for a in range(PASSES)]
+        w_raw = {
+            (b, a): keep.tile([P, PACK, KP], F32, name=f"w_raw{b}{a}", tag=f"w_raw{b}{a}", align_bytes=64)
+            for b in range(BLOCKS)
+            for a in range(PASSES)
+        }
+        wp_raw = keep.tile([P, BLOCKS * 2 * H], U8, name="wp_raw", align_bytes=64)
+
+        def load_table(a):
+            nc.sync.dma_start(
+                out=tab_w[a][:].bitcast(I32),
+                in_=tab_words[a].rearrange("p c i -> p (c i)").bitcast(I32),
+            )
+
+        def load_w(b, a):
+            nc.sync.dma_start(
+                out=w_raw[b, a][:],
+                in_=w1[a * KP : (a + 1) * KP, b * KP : (b + 1) * KP].rearrange("(p j) c -> p j c", j=PACK),
+            )
+
+        nc.sync.dma_start(offs_sb[:], offs)
+        nc.sync.dma_start(out=b1_sb[:], in_=b1.rearrange("(b p t) -> p b t", p=P, t=PACK))
+        load_table(0)
+        for q in range(4):
+            nc.sync.dma_start(
+                out=tab_sc[32 * q : 32 * q + 4 * PASSES, :].bitcast(I32),
+                in_=tab_scales[:, 4 * q : 4 * q + 4, :].bitcast(I32),
+            )
+        load_w(0, 0)
+        load_table(1)
+        for q in range(4):
+            nc.sync.dma_start(
+                out=wp_sc_raw[32 * q : 32 * q + 4, :].bitcast(I32).rearrange("r (a c) -> r a c", a=BLOCKS),
+                in_=wp_scales[:, 4 * q : 4 * q + 4, :].bitcast(I32).rearrange("a r c -> r a c"),
+            )
+        nc.sync.dma_start(
+            out=wp_raw[:].bitcast(I32).rearrange("p (a c) -> p a c", a=BLOCKS),
+            in_=wp_words.bitcast(I32).rearrange("a p c -> p a c"),
+        )
+        load_w(0, 1)
+        load_table(2)
+        load_w(0, 2)
+        nc.sync.dma_start(pos1_sb[:], pos1)
+        nc.sync.dma_start(pos2_sb[:], pos2)
+        nc.sync.dma_start(out=gd_sb[:], in_=gd.rearrange("(b p t) -> p b t", p=P, t=PACK))
+        for a in range(PASSES):
+            load_w(1, a)
+
+        v_codes = [keep.tile([P, S], U32, name=f"v_codes{a}", align_bytes=64) for a in range(PASSES)]
+        v_scales = keep.tile([P, S], U8, name="v_scales", align_bytes=64)
+        w_codes = {}
+        w_scales = {}
+        w_bf = {}
+
+        def gather_table(a):
+            nc.vector.tensor_copy(v_codes[a][:], tab_w[a][:].indirect(offs_sb[:]))
+
+        def cast_w(b, a, on_scalar):
+            w_bf[b, a] = keep.tile([P, PACK, P, PACK], BF16, name=f"w_bf{b}{a}", tag=f"w_bf{a}", align_bytes=64)
+            dst = w_bf[b, a][:].rearrange("p t m j -> p m t j")
+            src = w_raw[b, a][:].rearrange("p j (m t) -> p m t j", t=PACK)
+            if on_scalar > 0:
+                nc.scalar.activation(dst[:, :on_scalar], src[:, :on_scalar], ACT.Copy)
+            if on_scalar < P:
+                nc.vector.tensor_copy(dst[:, on_scalar:], src[:, on_scalar:])
+
+        def quantize_w(b, a):
+            w_codes[b, a] = keep.tile([P, KP], U32, name=f"w_codes{b}{a}", tag=f"w_codes{b}{a}", align_bytes=64)
+            w_scales[b, a] = keep.tile([P, KP], U8, name=f"w_scales{b}{a}", align_bytes=64)
+            nc.vector.quantize_mx(
+                out=w_codes[b, a][:].bitcast(FP8X4),
+                scales=w_scales[b, a][:],
+                in_=w_bf[b, a][:].rearrange("p t m j -> p (t m j)"),
+            )
+
+        banks = {}
+
+        def first_product(b, passes):
+            for t in range(PACK):
+              for a in passes:
+                for half in range(HALVES):
+                    if a == 0:
+                        banks[b, t, half] = psum.tile([P, BANK], F32, name=f"bank{HALVES * t + half}")
+                    cols = slice(half * BANK, (half + 1) * BANK)
+                    nc.tensor.matmul_mx(
+                        out=banks[b, t, half][:],
+                        lhsT=w_codes[b, a][:, t * P : (t + 1) * P].bitcast(FP8X4),
+                        lhsT_scale=w_scales[b, a][:, t * P : (t + 1) * P],
+                        rhs=v_codes[a][:, cols].bitcast(FP8X4),
+                        rhs_scale=v_scales[4 * a : P, cols],
+                        start=(a == 0),
+                        stop=(a == PASSES - 1),
+                    )
+
+        h = {}
+
+        def empty_h(b, t):
+            h[b, t] = keep.tile([P, S], F32, name=f"h{b}{t}")
+            for half in range(HALVES):
+                nc.scalar.activation(
+                    h[b, t][:, half * BANK : (half + 1) * BANK],
+                    banks[b, t, half][:],
+                    ACT.Identity,
+                    bias=b1_sb[:, b, t : t + 1],
+                )
+
+        up = {}
+        down = {}
+
+        def gather_up(b, t):
+            if t == 0:
+                up[b] = keep.tile([P, PACK, M], F32, name=f"up{b}", tag=("w_raw11", "up1")[b], align_bytes=64)
+            nc.vector.tensor_copy(up[b][:, t, :], h[b, t][:].indirect(pos1_sb[:]))
+
+        def gather_down(b, t):
+            nc.vector.tensor_copy(down[b, t], h[b, t][:].indirect(pos2_sb[:]))
+
+        x_bf = {}
+        x_codes = {}
+        x_scales = {}
+
+        def round_x(b):
+            x_bf[b] = keep.tile([P, M, PACK], BF16, name=f"x_bf{b}", tag=("w_raw12", "x_bf1")[b], align_bytes=64)
+            nc.scalar.activation(
+                x_bf[b][:].rearrange("p (c i) t -> p c t i", i=4),
+                up[b][:].rearrange("p t (c i) -> p c t i", i=4),
+                ACT.Abs,
+            )
+
+        def quantize_x(b):
+            x_codes[b] = keep.tile([P, M], U32, name=f"x_codes{b}", tag=f"x_codes{b}", align_bytes=64)
+            x_scales[b] = keep.tile([P, M], U8, name=f"x_scales{b}", align_bytes=64)
+            nc.vector.quantize_mx(
+                out=x_codes[b][:].bitcast(FP8X4),
+                scales=x_scales[b][:],
+                in_=x_bf[b][:].rearrange("p m t -> p (m t)"),
+            )
+
+        wp_codes = keep.tile([P, BLOCKS * 2 * H], U8, name="wp_codes", align_bytes=64)
+        wp_sc = keep.tile([P, BLOCKS * H], U8, name="wp_sc", align_bytes=64)
+
+        y = {}
+
+        def second_product(a):
+            for b in range(BLOCKS):
+                for t in range(PACK):
+                    if a == 0:
+                        y[b, t] = psum.tile([P, BANK], F32, name=f"bank{PACK * b + t}")
+                    c0 = a * H + b * KP + t * P
+                    nc.tensor.matmul_mx(
+                        out=y[b, t][:],
+                        lhsT=wp_codes[:, 2 * c0 : 2 * (c0 + P)].bitcast(FP4X4),
+                        lhsT_scale=wp_sc[:, c0 : c0 + P],
+                        rhs=x_codes[a][:].bitcast(FP8X4),
+                        rhs_scale=x_scales[a][:],
+                        start=(a == 0),
+                        stop=(a == BLOCKS - 1),
+                    )
+
+        gather_table(0)
+        nc.vector.tensor_copy(v_scales[:], tab_sc[:].indirect(offs_sb[:]))
+        cast_w(0, 0, P)
+        quantize_w(0, 0)
+        first_product(0, [0])
+        gather_table(1)
+        nc.vector.tensor_copy(
+            wp_codes[:].bitcast(U16).rearrange("p (g t m) -> p g t m", t=PACK, m=P),
+            wp_raw[:].bitcast(U16).rearrange("p (g m t) -> p g t m", t=PACK, m=P),
+        )
+        nc.vector.tensor_copy(
+            wp_sc[:].rearrange("p (g t m) -> p g t m", t=PACK, m=P),
+            wp_sc_raw[:].rearrange("p (g m t) -> p g t m", t=PACK, m=P),
+        )
+        cast_w(0, 1, P)
+        quantize_w(0, 1)
+        first_product(0, [1])
+        gather_table(2)
+        cast_w(0, 2, SCALAR_SHARE)
+        quantize_w(0, 2)
+        first_product(0, [2])
+        for t in range(PACK):
+            empty_h(0, t)
+        cast_w(1, 0, 0)
+        quantize_w(1, 0)
+        first_product(1, [0])
+        cast_w(1, 1, 0)
+        gather_up(0, 0)
+        quantize_w(1, 1)
+        gather_up(0, 1)
+        cast_w(1, 2, LAST_SHARE)
+        gather_up(0, 2)
+        gather_up(0, 3)
+        quantize_w(1, 2)
+        first_product(1, [1, 2])
+        round_x(0)
+        for t in range(PACK):
+            empty_h(1, t)
+            gather_up(1, t)
+        slices = [(b, t) for b in range(BLOCKS) for t in range(PACK)]
+
+        def gather_down_into(first, count, tag, align):
+            tile = keep.tile([P, count, M], F32, name=f"down{first}", tag=tag, align_bytes=align)
+            for i in range(count):
+                down[slices[first + i]] = tile[:, i, :]
+                gather_down(*slices[first + i])
+
+        gather_down_into(0, 1, "w_bf2", 64)
+        quantize_x(0)
+        second_product(0)
+        gather_down_into(1, 2, "x_codes0", 64)
+        round_x(1)
+        quantize_x(1)
+        second_product(1)
+        gather_down_into(3, 4, "up1", 64)
+        gather_down_into(7, 1, "x_bf1", 64)
+
+        mag = {}
+        damp = [keep.tile([P, PACK, M], F32, name=f"damp{b}", tag=f"w_raw0{b}", align_bytes=64) for b in range(BLOCKS)]
+        res = [keep.tile([P, PACK, M], F32, name=f"res{b}", tag=("w_raw02", "w_raw10")[b], align_bytes=64) for b in range(BLOCKS)]
+        roots = [keep.tile([P, PACK, M], F32, name=f"root{b}", tag=f"w_raw1{b + 1}", align_bytes=64) for b in range(BLOCKS)]
+        n = len(slices)
+        for step in range(n + 3):
+            if step < n:
+                mag[step] = ring.tile([P, M], F32, name="mag")
+                nc.scalar.activation(mag[step][:], y[slices[step]][:], ACT.Abs)
+            if 0 <= step - 1 < n:
+                b, t = slices[step - 1]
+                nc.scalar.activation(roots[b][:, t, :], mag[step - 1][:], ACT.Abs_reciprocal_sqrt, bias=1.0)
+            if 0 <= step - 2 < n:
+                b, t = slices[step - 2]
+                if step - 2 < SQUARES_ON_SCALAR:
+                    nc.scalar.activation(damp[b][:, t, :], roots[b][:, t, :], ACT.Square)
+                else:
+                    nc.vector.scalar_tensor_tensor(
+                        damp[b][:, t, :], roots[b][:, t, :], gd_sb[:, b, t : t + 1], down[b, t], MULT, MULT
+                    )
+            if 0 <= step - 3:
+                b, t = slices[step - 3]
+                if step - 3 < SQUARES_ON_SCALAR:
+                    nc.vector.scalar_tensor_tensor(
+                        res[b][:, t, :], damp[b][:, t, :], gd_sb[:, b, t : t + 1], down[b, t], MULT, MULT
+                    )
+                else:
+                    nc.vector.tensor_tensor(res[b][:, t, :], damp[b][:, t, :], roots[b][:, t, :], MULT)
+                nc.sync.dma_start(
+                    out=out[b * KP : (b + 1) * KP, :].rearrange("(p t) m -> p t m", t=PACK)[:, t, :],
+                    in_=res[b][:, t, :],
+                )

@@ -25,8 +25,8 @@ PASSES = K // KP
 BLOCKS = H // KP
 HALVES = S // BANK
 SCALAR_SHARE = 40
-LAST_SHARE = 128
-SQUARES_ON_SCALAR = 6
+LAST_SHARE = 64
+SQUARED_ON_VECTOR = 6
 
 
 def tile_list_cocoa_supply_tiers_kernel(
@@ -43,7 +43,7 @@ def tile_list_cocoa_supply_tiers_kernel(
         pos1_sb = lists.tile([P, M // 16], U16, name="pos1_sb")
         pos2_sb = lists.tile([P, M // 16], U16, name="pos2_sb")
 
-        tab_sc = keep.tile([P, T], U8, name="tab_sc", align_bytes=64)
+        tab_sc = keep.tile([P, T], U8, name="tab_sc", tag="v_codes1", align_bytes=64)
         wp_sc_raw = keep.tile([P, BLOCKS * H], U8, name="wp_sc_raw", align_bytes=64)
         nc.vector.memset(tab_sc[:].bitcast(I32), 0)
         nc.vector.memset(wp_sc_raw[:].bitcast(I32), 0)
@@ -77,7 +77,7 @@ def tile_list_cocoa_supply_tiers_kernel(
         nc.sync.dma_start(out=b1_sb[:], in_=b1.rearrange("(b p t) -> p b t", p=P, t=PACK))
         load_table(0)
         for q in range(4):
-            nc.sync.dma_start(
+            nc.gpsimd.dma_start(
                 out=tab_sc[32 * q : 32 * q + 4 * PASSES, :].bitcast(I32),
                 in_=tab_scales[:, 4 * q : 4 * q + 4, :].bitcast(I32),
             )
@@ -101,13 +101,14 @@ def tile_list_cocoa_supply_tiers_kernel(
         for a in range(PASSES):
             load_w(1, a)
 
-        v_codes = [keep.tile([P, S], U32, name=f"v_codes{a}", align_bytes=64) for a in range(PASSES)]
+        v_codes = {}
         v_scales = keep.tile([P, S], U8, name="v_scales", align_bytes=64)
         w_codes = {}
         w_scales = {}
         w_bf = {}
 
         def gather_table(a):
+            v_codes[a] = keep.tile([P, S], U32, name=f"v_codes{a}", tag=f"v_codes{a}", align_bytes=64)
             nc.vector.tensor_copy(v_codes[a][:], tab_w[a][:].indirect(offs_sb[:]))
 
         def cast_w(b, a, on_scalar):
@@ -161,34 +162,33 @@ def tile_list_cocoa_supply_tiers_kernel(
 
         up = {}
         down = {}
+        x_bf = {}
+        x_codes = [keep.tile([P, M], U32, name=f"x_codes{b}", tag=f"x_codes{b}", align_bytes=64) for b in range(BLOCKS)]
+        x_scales = [keep.tile([P, M], U8, name=f"x_scales{b}", align_bytes=64) for b in range(BLOCKS)]
 
-        def gather_up(b, t):
+        def gather_up(b, t, m0, width, tag):
             if t == 0:
-                up[b] = keep.tile([P, PACK, M], F32, name=f"up{b}", tag=("w_raw11", "up1")[b], align_bytes=64)
-            nc.vector.tensor_copy(up[b][:, t, :], h[b, t][:].indirect(pos1_sb[:]))
+                up[b, m0] = keep.tile([P, PACK, width], F32, name=f"up{b}_{m0}", tag=tag, align_bytes=64)
+            nc.vector.tensor_copy(
+                up[b, m0][:, t, :], h[b, t][:].indirect(pos1_sb[:, m0 // 16 : (m0 + width) // 16])
+            )
 
         def gather_down(b, t):
             nc.vector.tensor_copy(down[b, t], h[b, t][:].indirect(pos2_sb[:]))
 
-        x_bf = {}
-        x_codes = {}
-        x_scales = {}
-
-        def round_x(b):
-            x_bf[b] = keep.tile([P, M, PACK], BF16, name=f"x_bf{b}", tag=("w_raw12", "x_bf1")[b], align_bytes=64)
+        def round_x(b, m0, width, tag):
+            x_bf[b, m0] = keep.tile([P, width, PACK], BF16, name=f"x_bf{b}_{m0}", tag=tag, align_bytes=64)
             nc.scalar.activation(
-                x_bf[b][:].rearrange("p (c i) t -> p c t i", i=4),
-                up[b][:].rearrange("p t (c i) -> p c t i", i=4),
+                x_bf[b, m0][:].rearrange("p (c i) t -> p c t i", i=4),
+                up[b, m0][:].rearrange("p t (c i) -> p c t i", i=4),
                 ACT.Abs,
             )
 
-        def quantize_x(b):
-            x_codes[b] = keep.tile([P, M], U32, name=f"x_codes{b}", tag=f"x_codes{b}", align_bytes=64)
-            x_scales[b] = keep.tile([P, M], U8, name=f"x_scales{b}", align_bytes=64)
+        def quantize_x(b, m0, width):
             nc.vector.quantize_mx(
-                out=x_codes[b][:].bitcast(FP8X4),
-                scales=x_scales[b][:],
-                in_=x_bf[b][:].rearrange("p m t -> p (m t)"),
+                out=x_codes[b][:, m0 : m0 + width].bitcast(FP8X4),
+                scales=x_scales[b][:, m0 : m0 + width],
+                in_=x_bf[b, m0][:].rearrange("p m t -> p (m t)"),
             )
 
         wp_codes = keep.tile([P, BLOCKS * 2 * H], U8, name="wp_codes", align_bytes=64)
@@ -235,39 +235,43 @@ def tile_list_cocoa_supply_tiers_kernel(
         first_product(0, [2])
         for t in range(PACK):
             empty_h(0, t)
+        half_m = M // 2
         cast_w(1, 0, 0)
         quantize_w(1, 0)
         first_product(1, [0])
         cast_w(1, 1, 0)
-        gather_up(0, 0)
+        gather_up(0, 0, 0, half_m, "w_raw11")
         quantize_w(1, 1)
-        gather_up(0, 1)
+        for t in range(1, PACK):
+            gather_up(0, t, 0, half_m, "w_raw11")
         cast_w(1, 2, LAST_SHARE)
-        gather_up(0, 2)
-        gather_up(0, 3)
         quantize_w(1, 2)
         first_product(1, [1, 2])
-        round_x(0)
+        round_x(0, 0, half_m, "w_raw12")
+        for t in range(PACK):
+            gather_up(0, t, half_m, half_m, "w_bf2")
         for t in range(PACK):
             empty_h(1, t)
-            gather_up(1, t)
+            gather_up(1, t, 0, M, "up1")
         slices = [(b, t) for b in range(BLOCKS) for t in range(PACK)]
 
-        def gather_down_into(first, count, tag, align):
-            tile = keep.tile([P, count, M], F32, name=f"down{first}", tag=tag, align_bytes=align)
+        def gather_down_into(first, count, tag):
+            tile = keep.tile([P, count, M], F32, name=f"down{first}", tag=tag, align_bytes=64)
             for i in range(count):
                 down[slices[first + i]] = tile[:, i, :]
                 gather_down(*slices[first + i])
 
-        gather_down_into(0, 1, "w_bf2", 64)
-        quantize_x(0)
+        round_x(0, half_m, half_m, "w_codes12")
+        quantize_x(0, 0, half_m)
+        quantize_x(0, half_m, half_m)
         second_product(0)
-        gather_down_into(1, 2, "x_codes0", 64)
-        round_x(1)
-        quantize_x(1)
+        round_x(1, 0, M, "x_bf1")
+        gather_down_into(0, 1, "w_codes12")
+        quantize_x(1, 0, M)
         second_product(1)
-        gather_down_into(3, 4, "up1", 64)
-        gather_down_into(7, 1, "x_bf1", 64)
+        gather_down_into(1, 4, "up1")
+        gather_down_into(5, 2, "x_bf1")
+        gather_down_into(7, 1, "x_codes0")
 
         mag = {}
         damp = [keep.tile([P, PACK, M], F32, name=f"damp{b}", tag=f"w_raw0{b}", align_bytes=64) for b in range(BLOCKS)]
@@ -283,7 +287,7 @@ def tile_list_cocoa_supply_tiers_kernel(
                 nc.scalar.activation(roots[b][:, t, :], mag[step - 1][:], ACT.Abs_reciprocal_sqrt, bias=1.0)
             if 0 <= step - 2 < n:
                 b, t = slices[step - 2]
-                if step - 2 < SQUARES_ON_SCALAR:
+                if step - 2 != SQUARED_ON_VECTOR:
                     nc.scalar.activation(damp[b][:, t, :], roots[b][:, t, :], ACT.Square)
                 else:
                     nc.vector.scalar_tensor_tensor(
@@ -291,7 +295,7 @@ def tile_list_cocoa_supply_tiers_kernel(
                     )
             if 0 <= step - 3:
                 b, t = slices[step - 3]
-                if step - 3 < SQUARES_ON_SCALAR:
+                if step - 3 != SQUARED_ON_VECTOR:
                     nc.vector.scalar_tensor_tensor(
                         res[b][:, t, :], damp[b][:, t, :], gd_sb[:, b, t : t + 1], down[b, t], MULT, MULT
                     )

@@ -73,9 +73,9 @@ def tile_list_cocoa_supply_tiers_kernel(
                 in_=w1[a * KP : (a + 1) * KP, b * KP : (b + 1) * KP].rearrange("(p j) c -> p j c", j=PACK),
             )
 
+        load_table(0)
         nc.sync.dma_start(offs_sb[:], offs)
         nc.sync.dma_start(out=b1_sb[:], in_=b1.rearrange("(b p t) -> p b t", p=P, t=PACK))
-        load_table(0)
         for q in range(4):
             nc.gpsimd.dma_start(
                 out=tab_sc[32 * q : 32 * q + 4 * PASSES, :].bitcast(I32),
@@ -113,8 +113,8 @@ def tile_list_cocoa_supply_tiers_kernel(
 
         def cast_w(b, a, on_scalar):
             w_bf[b, a] = keep.tile([P, PACK, P, PACK], BF16, name=f"w_bf{b}{a}", tag=f"w_bf{a}", align_bytes=64)
-            dst = w_bf[b, a][:].rearrange("p t m j -> p m t j")
-            src = w_raw[b, a][:].rearrange("p j (m t) -> p m t j", t=PACK)
+            dst = w_bf[b, a][:].rearrange("p t m j -> p m j t")
+            src = w_raw[b, a][:].rearrange("p j (m t) -> p m j t", t=PACK)
             if on_scalar > 0:
                 nc.scalar.activation(dst[:, :on_scalar], src[:, :on_scalar], ACT.Copy)
             if on_scalar < P:
@@ -273,6 +273,9 @@ def tile_list_cocoa_supply_tiers_kernel(
         gather_down_into(5, 2, "x_bf1")
         gather_down_into(7, 1, "x_codes0")
 
+        def parts(k):
+            return [slice(0, M // 2), slice(M // 2, M)] if k == len(slices) - 1 else [slice(0, M)]
+
         mag = {}
         damp = [keep.tile([P, PACK, M], F32, name=f"damp{b}", tag=f"w_raw0{b}", align_bytes=64) for b in range(BLOCKS)]
         res = [keep.tile([P, PACK, M], F32, name=f"res{b}", tag=("w_raw02", "w_raw10")[b], align_bytes=64) for b in range(BLOCKS)]
@@ -287,21 +290,23 @@ def tile_list_cocoa_supply_tiers_kernel(
                 nc.scalar.activation(roots[b][:, t, :], mag[step - 1][:], ACT.Abs_reciprocal_sqrt, bias=1.0)
             if 0 <= step - 2 < n:
                 b, t = slices[step - 2]
-                if step - 2 != SQUARED_ON_VECTOR:
-                    nc.scalar.activation(damp[b][:, t, :], roots[b][:, t, :], ACT.Square)
-                else:
+                if step - 2 == SQUARED_ON_VECTOR:
                     nc.vector.scalar_tensor_tensor(
                         damp[b][:, t, :], roots[b][:, t, :], gd_sb[:, b, t : t + 1], down[b, t], MULT, MULT
                     )
+                else:
+                    for cols in parts(step - 2):
+                        nc.scalar.activation(damp[b][:, t, cols], roots[b][:, t, cols], ACT.Square)
             if 0 <= step - 3:
                 b, t = slices[step - 3]
-                if step - 3 != SQUARED_ON_VECTOR:
-                    nc.vector.scalar_tensor_tensor(
-                        res[b][:, t, :], damp[b][:, t, :], gd_sb[:, b, t : t + 1], down[b, t], MULT, MULT
+                for cols in parts(step - 3):
+                    if step - 3 == SQUARED_ON_VECTOR:
+                        nc.vector.tensor_tensor(res[b][:, t, :], damp[b][:, t, :], roots[b][:, t, :], MULT)
+                    else:
+                        nc.vector.scalar_tensor_tensor(
+                            res[b][:, t, cols], damp[b][:, t, cols], gd_sb[:, b, t : t + 1], down[b, t][:, cols], MULT, MULT
+                        )
+                    nc.sync.dma_start(
+                        out=out[b * KP : (b + 1) * KP, :].rearrange("(p t) m -> p t m", t=PACK)[:, t, cols],
+                        in_=res[b][:, t, cols],
                     )
-                else:
-                    nc.vector.tensor_tensor(res[b][:, t, :], damp[b][:, t, :], roots[b][:, t, :], MULT)
-                nc.sync.dma_start(
-                    out=out[b * KP : (b + 1) * KP, :].rearrange("(p t) m -> p t m", t=PACK)[:, t, :],
-                    in_=res[b][:, t, :],
-                )

@@ -14,8 +14,7 @@ U8 = mybir.dt.uint8
 FP8X4 = mybir.dt.float8_e4m3fn_x4
 FP4X4 = mybir.dt.float4_e2m1fn_x4
 ACT = mybir.ActivationFunctionType
-MULT = mybir.AluOpType.mult
-ADD = mybir.AluOpType.add
+ALU = mybir.AluOpType
 
 P = 128
 PACK = 4
@@ -24,9 +23,11 @@ BANK = 512
 PASSES = K // KP
 BLOCKS = H // KP
 HALVES = S // BANK
-SCALAR_SHARE = 40
-LAST_SHARE = 64
-SQUARED_ON_VECTOR = 6
+HALF_M = M // 2
+SLICES = [(b, t) for b in range(BLOCKS) for t in range(PACK)]
+SMALLEST_NORMAL = 2.0**-126
+FUSED = 0
+SQUARED_ON_VECTOR = ()
 
 
 def tile_list_cocoa_supply_tiers_kernel(
@@ -39,27 +40,22 @@ def tile_list_cocoa_supply_tiers_kernel(
         ring = ctx.enter_context(tc.tile_pool(name="ring", bufs=3))
         psum = ctx.enter_context(tc.psum_pool(name="psum", bufs=1))
 
+        def tile(name, shape, dtype, tag=None):
+            return keep.tile(shape, dtype, name=name, tag=tag or name, align_bytes=64)
+
         offs_sb = lists.tile([P, S // 16], U16, name="offs_sb")
         pos1_sb = lists.tile([P, M // 16], U16, name="pos1_sb")
         pos2_sb = lists.tile([P, M // 16], U16, name="pos2_sb")
 
-        tab_sc = keep.tile([P, T], U8, name="tab_sc", tag="v_codes1", align_bytes=64)
-        wp_sc_raw = keep.tile([P, BLOCKS * H], U8, name="wp_sc_raw", align_bytes=64)
+        tab_sc = tile("tab_sc", [P, T], U8)
+        wp_sc_raw = tile("wp_sc_raw", [P, BLOCKS * H], U8)
         nc.vector.memset(tab_sc[:].bitcast(I32), 0)
         nc.vector.memset(wp_sc_raw[:].bitcast(I32), 0)
-        warm = keep.tile([P, 8], F32, name="warm")
-        nc.vector.memset(warm[:, 0:1], 1.0)
-        nc.scalar.activation(warm[:, 1:2], warm[:, 0:1], ACT.Abs_reciprocal_sqrt)
-        b1_sb = keep.tile([P, BLOCKS, PACK], F32, name="b1_sb")
-        gd_sb = keep.tile([P, BLOCKS, PACK], F32, name="gd_sb")
-
-        tab_w = [keep.tile([P, T], U32, name=f"tab_w{a}") for a in range(PASSES)]
-        w_raw = {
-            (b, a): keep.tile([P, PACK, KP], F32, name=f"w_raw{b}{a}", tag=f"w_raw{b}{a}", align_bytes=64)
-            for b in range(BLOCKS)
-            for a in range(PASSES)
-        }
-        wp_raw = keep.tile([P, BLOCKS * 2 * H], U8, name="wp_raw", align_bytes=64)
+        b1_sb = tile("b1_sb", [P, BLOCKS, PACK], F32)
+        gd_sb = tile("gd_sb", [P, BLOCKS, PACK], F32)
+        tab_w = [tile(f"tab_w{a}", [P, T], U32) for a in range(PASSES)]
+        w_raw = {(b, a): tile(f"w_raw{b}{a}", [P, PACK, KP], F32) for b in range(BLOCKS) for a in range(PASSES)}
+        wp_raw = tile("wp_raw", [P, BLOCKS * 2 * H], U8)
 
         def load_table(a):
             nc.sync.dma_start(
@@ -73,46 +69,71 @@ def tile_list_cocoa_supply_tiers_kernel(
                 in_=w1[a * KP : (a + 1) * KP, b * KP : (b + 1) * KP].rearrange("(p j) c -> p j c", j=PACK),
             )
 
-        load_table(0)
+        def load_wp_scales(q):
+            nc.sync.dma_start(
+                out=wp_sc_raw[32 * q : 32 * q + 4, :].bitcast(I32).rearrange("r (a c) -> r a c", a=BLOCKS),
+                in_=wp_scales[:, 4 * q : 4 * q + 4, :].bitcast(I32).rearrange("a r c -> r a c"),
+            )
+
+        nc.sync.dma_start(out=gd_sb[:], in_=gd.rearrange("(b p t) -> p b t", p=P, t=PACK))
         nc.sync.dma_start(offs_sb[:], offs)
-        nc.sync.dma_start(out=b1_sb[:], in_=b1.rearrange("(b p t) -> p b t", p=P, t=PACK))
+        load_table(0)
         for q in range(4):
             nc.gpsimd.dma_start(
                 out=tab_sc[32 * q : 32 * q + 4 * PASSES, :].bitcast(I32),
                 in_=tab_scales[:, 4 * q : 4 * q + 4, :].bitcast(I32),
             )
         load_w(0, 0)
-        load_table(1)
-        for q in range(4):
-            nc.sync.dma_start(
-                out=wp_sc_raw[32 * q : 32 * q + 4, :].bitcast(I32).rearrange("r (a c) -> r a c", a=BLOCKS),
-                in_=wp_scales[:, 4 * q : 4 * q + 4, :].bitcast(I32).rearrange("a r c -> r a c"),
-            )
+        load_w(0, 1)
         nc.sync.dma_start(
             out=wp_raw[:].bitcast(I32).rearrange("p (a c) -> p a c", a=BLOCKS),
             in_=wp_words.bitcast(I32).rearrange("a p c -> p a c"),
         )
-        load_w(0, 1)
-        load_table(2)
-        load_w(0, 2)
+        nc.sync.dma_start(out=b1_sb[:], in_=b1.rearrange("(b p t) -> p b t", p=P, t=PACK))
         nc.sync.dma_start(pos1_sb[:], pos1)
         nc.sync.dma_start(pos2_sb[:], pos2)
-        nc.sync.dma_start(out=gd_sb[:], in_=gd.rearrange("(b p t) -> p b t", p=P, t=PACK))
+        for q in range(2):
+            load_wp_scales(q)
+        load_table(1)
+        for q in range(2, 4):
+            load_wp_scales(q)
+        load_w(0, 2)
+        load_table(2)
         for a in range(PASSES):
             load_w(1, a)
 
+        gd_abs = tile("gd_abs", [P, BLOCKS, PACK], F32)
+        gd_floor = tile("gd_floor", [P, BLOCKS, PACK], F32)
+        gd_rsqrt = tile("gd_rsqrt", [P, BLOCKS, PACK], F32)
+        gd_root = tile("gd_root", [P, BLOCKS, PACK], F32)
+        positive = tile("positive", [P, BLOCKS, PACK], F32)
+        sign = tile("sign", [P, BLOCKS, PACK], F32)
+        b1_signed = tile("b1_signed", [P, BLOCKS, PACK], F32)
+        nc.vector.tensor_scalar(positive[:], gd_sb[:], 0.0, None, ALU.is_ge)
+        nc.vector.tensor_scalar(sign[:], positive[:], 2.0, -1.0, ALU.mult, ALU.add)
+        nc.vector.tensor_tensor(gd_abs[:], gd_sb[:], sign[:], ALU.mult)
+        nc.vector.tensor_tensor(b1_signed[:], b1_sb[:], sign[:], ALU.mult)
+        nc.vector.tensor_scalar(gd_floor[:], gd_abs[:], SMALLEST_NORMAL, None, ALU.max)
+        nc.scalar.activation(gd_rsqrt[:], gd_floor[:], ACT.Abs_reciprocal_sqrt)
+        nc.vector.tensor_tensor(gd_root[:], gd_abs[:], gd_rsqrt[:], ALU.mult)
+
         v_codes = {}
-        v_scales = keep.tile([P, S], U8, name="v_scales", align_bytes=64)
+        v_scales = tile("v_scales", [P, S], U8)
         w_codes = {}
         w_scales = {}
         w_bf = {}
 
-        def gather_table(a):
-            v_codes[a] = keep.tile([P, S], U32, name=f"v_codes{a}", tag=f"v_codes{a}", align_bytes=64)
-            nc.vector.tensor_copy(v_codes[a][:], tab_w[a][:].indirect(offs_sb[:]))
+        def gather_table(a, halves):
+            first, count = halves[0], len(halves)
+            picked = tile(f"v_codes{a}{first}", [P, count * BANK], U32)
+            nc.vector.tensor_copy(
+                picked[:], tab_w[a][:].indirect(offs_sb[:, first * BANK // 16 : (first + count) * BANK // 16])
+            )
+            for i, half in enumerate(halves):
+                v_codes[a, half] = picked[:, i * BANK : (i + 1) * BANK]
 
         def cast_w(b, a, on_scalar):
-            w_bf[b, a] = keep.tile([P, PACK, P, PACK], BF16, name=f"w_bf{b}{a}", tag=f"w_bf{a}", align_bytes=64)
+            w_bf[b, a] = tile(f"w_bf{b}{a}", [P, PACK, P, PACK], BF16, tag=f"w_bf{a}")
             dst = w_bf[b, a][:].rearrange("p t m j -> p m j t")
             src = w_raw[b, a][:].rearrange("p j (m t) -> p m j t", t=PACK)
             if on_scalar > 0:
@@ -121,8 +142,8 @@ def tile_list_cocoa_supply_tiers_kernel(
                 nc.vector.tensor_copy(dst[:, on_scalar:], src[:, on_scalar:])
 
         def quantize_w(b, a):
-            w_codes[b, a] = keep.tile([P, KP], U32, name=f"w_codes{b}{a}", tag=f"w_codes{b}{a}", align_bytes=64)
-            w_scales[b, a] = keep.tile([P, KP], U8, name=f"w_scales{b}{a}", align_bytes=64)
+            w_codes[b, a] = tile(f"w_codes{b}{a}", [P, KP], U32)
+            w_scales[b, a] = tile(f"w_scales{b}{a}", [P, KP], U8)
             nc.vector.quantize_mx(
                 out=w_codes[b, a][:].bitcast(FP8X4),
                 scales=w_scales[b, a][:],
@@ -131,93 +152,84 @@ def tile_list_cocoa_supply_tiers_kernel(
 
         banks = {}
 
-        def first_product(b, passes):
-            for t in range(PACK):
-              for a in passes:
-                for half in range(HALVES):
-                    if a == 0:
-                        banks[b, t, half] = psum.tile([P, BANK], F32, name=f"bank{HALVES * t + half}")
-                    cols = slice(half * BANK, (half + 1) * BANK)
-                    nc.tensor.matmul_mx(
-                        out=banks[b, t, half][:],
-                        lhsT=w_codes[b, a][:, t * P : (t + 1) * P].bitcast(FP8X4),
-                        lhsT_scale=w_scales[b, a][:, t * P : (t + 1) * P],
-                        rhs=v_codes[a][:, cols].bitcast(FP8X4),
-                        rhs_scale=v_scales[4 * a : P, cols],
-                        start=(a == 0),
-                        stop=(a == PASSES - 1),
-                    )
-
-        h = {}
-
-        def empty_h(b, t):
-            h[b, t] = keep.tile([P, S], F32, name=f"h{b}{t}")
-            for half in range(HALVES):
-                nc.scalar.activation(
-                    h[b, t][:, half * BANK : (half + 1) * BANK],
-                    banks[b, t, half][:],
-                    ACT.Identity,
-                    bias=b1_sb[:, b, t : t + 1],
+        def first_product(b, a, order):
+            for t, half in order:
+                if a == 0:
+                    banks[b, t, half] = psum.tile([P, BANK], F32, name=f"bank{HALVES * t + half}")
+                nc.tensor.matmul_mx(
+                    out=banks[b, t, half][:],
+                    lhsT=w_codes[b, a][:, t * P : (t + 1) * P].bitcast(FP8X4),
+                    lhsT_scale=w_scales[b, a][:, t * P : (t + 1) * P],
+                    rhs=v_codes[a, half].bitcast(FP8X4),
+                    rhs_scale=v_scales[4 * a : P, half * BANK : (half + 1) * BANK],
+                    start=(a == 0),
+                    stop=(a == PASSES - 1),
                 )
 
-        up = {}
-        down = {}
-        x_bf = {}
-        x_codes = [keep.tile([P, M], U32, name=f"x_codes{b}", tag=f"x_codes{b}", align_bytes=64) for b in range(BLOCKS)]
-        x_scales = [keep.tile([P, M], U8, name=f"x_scales{b}", align_bytes=64) for b in range(BLOCKS)]
+        h = {(b, t): tile(f"h{b}{t}", [P, S], F32) for b, t in SLICES}
 
-        def gather_up(b, t, m0, width, tag):
-            if t == 0:
-                up[b, m0] = keep.tile([P, PACK, width], F32, name=f"up{b}_{m0}", tag=tag, align_bytes=64)
-            nc.vector.tensor_copy(
-                up[b, m0][:, t, :], h[b, t][:].indirect(pos1_sb[:, m0 // 16 : (m0 + width) // 16])
+        def empty_h(b, t, half):
+            nc.scalar.activation(
+                h[b, t][:, half * BANK : (half + 1) * BANK],
+                banks[b, t, half][:],
+                ACT.Identity,
+                bias=b1_signed[:, b, t : t + 1],
+                scale=sign[:, b, t : t + 1],
             )
 
-        def gather_down(b, t):
-            nc.vector.tensor_copy(down[b, t], h[b, t][:].indirect(pos2_sb[:]))
+        x_codes = [tile(f"x_codes{b}", [P, M], U32) for b in range(BLOCKS)]
+        x_scales = [tile(f"x_scales{b}", [P, M], U8) for b in range(BLOCKS)]
 
-        def round_x(b, m0, width, tag):
-            x_bf[b, m0] = keep.tile([P, width, PACK], BF16, name=f"x_bf{b}_{m0}", tag=tag, align_bytes=64)
+        def gather_up(dst, b, t, m0, width):
+            nc.vector.tensor_copy(dst, h[b, t][:].indirect(pos1_sb[:, m0 // 16 : (m0 + width) // 16]))
+
+        def round_x(name, up, tag):
+            x_bf = tile(name, [P, HALF_M, PACK], BF16, tag=tag)
             nc.scalar.activation(
-                x_bf[b, m0][:].rearrange("p (c i) t -> p c t i", i=4),
-                up[b, m0][:].rearrange("p t (c i) -> p c t i", i=4),
+                x_bf[:].rearrange("p (c i) t -> p c t i", i=4),
+                up.rearrange("p t (c i) -> p c t i", i=4),
                 ACT.Abs,
             )
+            return x_bf
 
-        def quantize_x(b, m0, width):
+        def quantize_x(b, m0, x_bf):
             nc.vector.quantize_mx(
-                out=x_codes[b][:, m0 : m0 + width].bitcast(FP8X4),
-                scales=x_scales[b][:, m0 : m0 + width],
-                in_=x_bf[b, m0][:].rearrange("p m t -> p (m t)"),
+                out=x_codes[b][:, m0 : m0 + HALF_M].bitcast(FP8X4),
+                scales=x_scales[b][:, m0 : m0 + HALF_M],
+                in_=x_bf[:].rearrange("p m t -> p (m t)"),
             )
 
-        wp_codes = keep.tile([P, BLOCKS * 2 * H], U8, name="wp_codes", align_bytes=64)
-        wp_sc = keep.tile([P, BLOCKS * H], U8, name="wp_sc", align_bytes=64)
-
+        wp_codes = tile("wp_codes", [P, BLOCKS * 2 * H], U8)
+        wp_sc = tile("wp_sc", [P, BLOCKS * H], U8)
         y = {}
 
         def second_product(a):
-            for b in range(BLOCKS):
-                for t in range(PACK):
-                    if a == 0:
-                        y[b, t] = psum.tile([P, BANK], F32, name=f"bank{PACK * b + t}")
-                    c0 = a * H + b * KP + t * P
-                    nc.tensor.matmul_mx(
-                        out=y[b, t][:],
-                        lhsT=wp_codes[:, 2 * c0 : 2 * (c0 + P)].bitcast(FP4X4),
-                        lhsT_scale=wp_sc[:, c0 : c0 + P],
-                        rhs=x_codes[a][:].bitcast(FP8X4),
-                        rhs_scale=x_scales[a][:],
-                        start=(a == 0),
-                        stop=(a == BLOCKS - 1),
-                    )
+            for k, (b, t) in enumerate(SLICES):
+                if a == 0:
+                    y[b, t] = psum.tile([P, BANK], F32, name=f"bank{k}")
+                c0 = a * H + b * KP + t * P
+                nc.tensor.matmul_mx(
+                    out=y[b, t][:],
+                    lhsT=wp_codes[:, 2 * c0 : 2 * (c0 + P)].bitcast(FP4X4),
+                    lhsT_scale=wp_sc[:, c0 : c0 + P],
+                    rhs=x_codes[a][:].bitcast(FP8X4),
+                    rhs_scale=x_scales[a][:],
+                    start=(a == 0),
+                    stop=(a == BLOCKS - 1),
+                )
 
-        gather_table(0)
+        by_half = [(t, half) for half in range(HALVES) for t in range(PACK)]
+        by_slice = [(t, half) for t in range(PACK) for half in range(HALVES)]
+
+        gather_table(0, (0, 1))
         nc.vector.tensor_copy(v_scales[:], tab_sc[:].indirect(offs_sb[:]))
         cast_w(0, 0, P)
         quantize_w(0, 0)
-        first_product(0, [0])
-        gather_table(1)
+        first_product(0, 0, by_half)
+        cast_w(0, 1, P)
+        quantize_w(0, 1)
+        gather_table(1, (0, 1))
+        first_product(0, 1, by_half)
         nc.vector.tensor_copy(
             wp_codes[:].bitcast(U16).rearrange("p (g t m) -> p g t m", t=PACK, m=P),
             wp_raw[:].bitcast(U16).rearrange("p (g m t) -> p g t m", t=PACK, m=P),
@@ -226,87 +238,93 @@ def tile_list_cocoa_supply_tiers_kernel(
             wp_sc[:].rearrange("p (g t m) -> p g t m", t=PACK, m=P),
             wp_sc_raw[:].rearrange("p (g m t) -> p g t m", t=PACK, m=P),
         )
-        cast_w(0, 1, P)
-        quantize_w(0, 1)
-        first_product(0, [1])
-        gather_table(2)
-        cast_w(0, 2, SCALAR_SHARE)
+        cast_w(0, 2, P)
         quantize_w(0, 2)
-        first_product(0, [2])
+        gather_table(2, (0,))
+        gather_table(2, (1,))
+        first_product(0, 2, by_half)
+        for t, half in by_half:
+            empty_h(0, t, half)
+        for a in range(2):
+            cast_w(1, a, 0)
+            quantize_w(1, a)
+            first_product(1, a, by_half)
+        up_first = tile("up_first", [P, PACK, HALF_M], F32, tag="w_bf1")
         for t in range(PACK):
-            empty_h(0, t)
-        half_m = M // 2
-        cast_w(1, 0, 0)
-        quantize_w(1, 0)
-        first_product(1, [0])
-        cast_w(1, 1, 0)
-        gather_up(0, 0, 0, half_m, "w_raw11")
-        quantize_w(1, 1)
-        for t in range(1, PACK):
-            gather_up(0, t, 0, half_m, "w_raw11")
-        cast_w(1, 2, LAST_SHARE)
+            gather_up(up_first[:, t, :], 0, t, 0, HALF_M)
+        cast_w(1, 2, P)
         quantize_w(1, 2)
-        first_product(1, [1, 2])
-        round_x(0, 0, half_m, "w_raw12")
+        first_product(1, 2, by_slice)
+        x_first = round_x("x_first", up_first[:], "w_raw12")
+        up_second = tile("up_second", [P, PACK, HALF_M], F32, tag="w_bf2")
         for t in range(PACK):
-            gather_up(0, t, half_m, half_m, "w_bf2")
+            gather_up(up_second[:, t, :], 0, t, HALF_M, HALF_M)
+        quantize_x(0, 0, x_first)
+        up_last = tile("up_last", [P, PACK, M], F32)
         for t in range(PACK):
-            empty_h(1, t)
-            gather_up(1, t, 0, M, "up1")
-        slices = [(b, t) for b in range(BLOCKS) for t in range(PACK)]
-
-        def gather_down_into(first, count, tag):
-            tile = keep.tile([P, count, M], F32, name=f"down{first}", tag=tag, align_bytes=64)
-            for i in range(count):
-                down[slices[first + i]] = tile[:, i, :]
-                gather_down(*slices[first + i])
-
-        round_x(0, half_m, half_m, "w_codes12")
-        quantize_x(0, 0, half_m)
-        quantize_x(0, half_m, half_m)
+            for half in range(HALVES):
+                empty_h(1, t, half)
+            if t < PACK - 1:
+                gather_up(up_last[:, t, :], 1, t, 0, M)
+            else:
+                for m0 in (0, HALF_M):
+                    gather_up(up_last[:, t, m0 : m0 + HALF_M], 1, t, m0, HALF_M)
+        x_second = round_x("x_second", up_second[:], "w_codes12")
+        quantize_x(0, HALF_M, x_second)
         second_product(0)
-        round_x(1, 0, M, "x_bf1")
-        gather_down_into(0, 1, "w_codes12")
-        quantize_x(1, 0, M)
+        down = {}
+
+        def gather_down(name, ks, tag):
+            picked = tile(name, [P, len(ks), M], F32, tag=tag)
+            for i, k in enumerate(ks):
+                down[k] = picked[:, i, :]
+                nc.vector.tensor_copy(down[k], h[SLICES[k]][:].indirect(pos2_sb[:]))
+
+        plain = list(range(FUSED, len(SLICES)))
+        x_third = round_x("x_third", up_last[:, :, :HALF_M], "x_third")
+        x_fourth = round_x("x_fourth", up_last[:, :, HALF_M:], "x_fourth")
+        gather_down("down_early", plain[:1], "w_bf2")
+        quantize_x(1, 0, x_third)
+        quantize_x(1, HALF_M, x_fourth)
         second_product(1)
-        gather_down_into(1, 4, "up1")
-        gather_down_into(5, 2, "x_bf1")
-        gather_down_into(7, 1, "x_codes0")
+        gather_down("down_late", plain[1:], "x_fourth")
 
         def parts(k):
-            return [slice(0, M // 2), slice(M // 2, M)] if k == len(slices) - 1 else [slice(0, M)]
+            return [slice(0, HALF_M), slice(HALF_M, M)] if k == len(SLICES) - 1 else [slice(0, M)]
 
+        n = len(SLICES)
         mag = {}
-        damp = [keep.tile([P, PACK, M], F32, name=f"damp{b}", tag=f"w_raw0{b}", align_bytes=64) for b in range(BLOCKS)]
-        res = [keep.tile([P, PACK, M], F32, name=f"res{b}", tag=("w_raw02", "w_raw10")[b], align_bytes=64) for b in range(BLOCKS)]
-        roots = [keep.tile([P, PACK, M], F32, name=f"root{b}", tag=f"w_raw1{b + 1}", align_bytes=64) for b in range(BLOCKS)]
-        n = len(slices)
+        roots = tile("roots", [P, n, M], F32, tag="tab_w0")
+        damp = tile("damp", [P, n, M], F32, tag="tab_w1")
+        res = tile("res", [P, n, M], F32, tag="tab_w2")
         for step in range(n + 3):
             if step < n:
                 mag[step] = ring.tile([P, M], F32, name="mag")
-                nc.scalar.activation(mag[step][:], y[slices[step]][:], ACT.Abs)
-            if 0 <= step - 1 < n:
-                b, t = slices[step - 1]
-                nc.scalar.activation(roots[b][:, t, :], mag[step - 1][:], ACT.Abs_reciprocal_sqrt, bias=1.0)
-            if 0 <= step - 2 < n:
-                b, t = slices[step - 2]
-                if step - 2 == SQUARED_ON_VECTOR:
+                nc.scalar.activation(mag[step][:], y[SLICES[step]][:], ACT.Abs)
+            k = step - 1
+            if 0 <= k < n:
+                nc.scalar.activation(roots[:, k, :], mag[k][:], ACT.Abs_reciprocal_sqrt, bias=1.0)
+            k = step - 2
+            if 0 <= k < n:
+                b, t = SLICES[k]
+                if k in SQUARED_ON_VECTOR:
                     nc.vector.scalar_tensor_tensor(
-                        damp[b][:, t, :], roots[b][:, t, :], gd_sb[:, b, t : t + 1], down[b, t], MULT, MULT
+                        damp[:, k, :], roots[:, k, :], gd_abs[:, b, t : t + 1], roots[:, k, :], ALU.mult, ALU.mult
                     )
                 else:
-                    for cols in parts(step - 2):
-                        nc.scalar.activation(damp[b][:, t, cols], roots[b][:, t, cols], ACT.Square)
-            if 0 <= step - 3:
-                b, t = slices[step - 3]
-                for cols in parts(step - 3):
-                    if step - 3 == SQUARED_ON_VECTOR:
-                        nc.vector.tensor_tensor(res[b][:, t, :], damp[b][:, t, :], roots[b][:, t, :], MULT)
-                    else:
-                        nc.vector.scalar_tensor_tensor(
-                            res[b][:, t, cols], damp[b][:, t, cols], gd_sb[:, b, t : t + 1], down[b, t][:, cols], MULT, MULT
+                    for cols in parts(k):
+                        nc.scalar.activation(
+                            damp[:, k, cols], roots[:, k, cols], ACT.Square, scale=gd_root[:, b, t : t + 1]
                         )
+            k = step - 3
+            if 0 <= k:
+                b, t = SLICES[k]
+                for cols in parts(k):
+                    if k < FUSED:
+                        nc.vector.tensor_tensor(res[:, k, :], h[b, t][:].indirect(pos2_sb[:]), damp[:, k, :], ALU.mult)
+                    else:
+                        nc.vector.tensor_tensor(res[:, k, cols], damp[:, k, cols], down[k][:, cols], ALU.mult)
                     nc.sync.dma_start(
                         out=out[b * KP : (b + 1) * KP, :].rearrange("(p t) m -> p t m", t=PACK)[:, t, cols],
-                        in_=res[b][:, t, cols],
+                        in_=res[:, k, cols],
                     )

@@ -26,8 +26,8 @@ HALVES = S // BANK
 HALF_M = M // 2
 SLICES = [(b, t) for b in range(BLOCKS) for t in range(PACK)]
 SMALLEST_NORMAL = 2.0**-126
-FUSED = 0
-SQUARED_ON_VECTOR = ()
+FUSED = 5
+SQUARED_ON_VECTOR = (0,1,2)
 
 
 def tile_list_cocoa_supply_tiers_kernel(

@@ -25,9 +25,10 @@ BLOCKS = H // KP
 HALVES = S // BANK
 HALF_M = M // 2
 SLICES = [(b, t) for b in range(BLOCKS) for t in range(PACK)]
+EARLY = 2
 SMALLEST_NORMAL = 2.0**-126
-FUSED = 5
-SQUARED_ON_VECTOR = (0,1,2)
+FUSED = 7
+SQUARED_ON_VECTOR = 2
 
 
 def tile_list_cocoa_supply_tiers_kernel(
@@ -37,20 +38,23 @@ def tile_list_cocoa_supply_tiers_kernel(
     with ExitStack() as ctx:
         lists = ctx.enter_context(tc.tile_pool(name="lists", bufs=1))
         keep = ctx.enter_context(tc.tile_pool(name="keep", bufs=1))
+        shared = ctx.enter_context(tc.tile_pool(name="shared", bufs=1))
         ring = ctx.enter_context(tc.tile_pool(name="ring", bufs=3))
         psum = ctx.enter_context(tc.psum_pool(name="psum", bufs=1))
 
         def tile(name, shape, dtype, tag=None):
+            if isinstance(tag, int):
+                return shared.tile(shape, dtype, name=name, offset=tag, align_bytes=64)
             return keep.tile(shape, dtype, name=name, tag=tag or name, align_bytes=64)
 
         offs_sb = lists.tile([P, S // 16], U16, name="offs_sb")
         pos1_sb = lists.tile([P, M // 16], U16, name="pos1_sb")
         pos2_sb = lists.tile([P, M // 16], U16, name="pos2_sb")
 
-        tab_sc = tile("tab_sc", [P, T], U8)
-        wp_sc_raw = tile("wp_sc_raw", [P, BLOCKS * H], U8)
-        nc.vector.memset(tab_sc[:].bitcast(I32), 0)
+        tab_sc = shared.tile([P, T], U8, name="tab_sc", offset=0, align_bytes=64)
+        wp_sc_raw = shared.tile([P, BLOCKS * H], U8, name="wp_sc_raw", offset=T, align_bytes=64)
         nc.vector.memset(wp_sc_raw[:].bitcast(I32), 0)
+        nc.vector.memset(tab_sc[:].bitcast(I32), 0)
         b1_sb = tile("b1_sb", [P, BLOCKS, PACK], F32)
         gd_sb = tile("gd_sb", [P, BLOCKS, PACK], F32)
         tab_w = [tile(f"tab_w{a}", [P, T], U32) for a in range(PASSES)]
@@ -75,7 +79,6 @@ def tile_list_cocoa_supply_tiers_kernel(
                 in_=wp_scales[:, 4 * q : 4 * q + 4, :].bitcast(I32).rearrange("a r c -> r a c"),
             )
 
-        nc.sync.dma_start(out=gd_sb[:], in_=gd.rearrange("(b p t) -> p b t", p=P, t=PACK))
         nc.sync.dma_start(offs_sb[:], offs)
         load_table(0)
         for q in range(4):
@@ -83,24 +86,23 @@ def tile_list_cocoa_supply_tiers_kernel(
                 out=tab_sc[32 * q : 32 * q + 4 * PASSES, :].bitcast(I32),
                 in_=tab_scales[:, 4 * q : 4 * q + 4, :].bitcast(I32),
             )
-        load_w(0, 0)
-        load_w(0, 1)
+        nc.sync.dma_start(out=gd_sb[:], in_=gd.rearrange("(b p t) -> p b t", p=P, t=PACK))
+        for a in range(PASSES):
+            load_w(0, a)
+        nc.sync.dma_start(out=b1_sb[:], in_=b1.rearrange("(b p t) -> p b t", p=P, t=PACK))
+        nc.sync.dma_start(pos1_sb[:], pos1)
+        for q in range(3):
+            load_wp_scales(q)
+        load_table(1)
+        load_wp_scales(3)
+        nc.sync.dma_start(pos2_sb[:], pos2)
+        load_table(2)
+        for a in range(PASSES):
+            load_w(1, a)
         nc.sync.dma_start(
             out=wp_raw[:].bitcast(I32).rearrange("p (a c) -> p a c", a=BLOCKS),
             in_=wp_words.bitcast(I32).rearrange("a p c -> p a c"),
         )
-        nc.sync.dma_start(out=b1_sb[:], in_=b1.rearrange("(b p t) -> p b t", p=P, t=PACK))
-        nc.sync.dma_start(pos1_sb[:], pos1)
-        nc.sync.dma_start(pos2_sb[:], pos2)
-        for q in range(2):
-            load_wp_scales(q)
-        load_table(1)
-        for q in range(2, 4):
-            load_wp_scales(q)
-        load_w(0, 2)
-        load_table(2)
-        for a in range(PASSES):
-            load_w(1, a)
 
         gd_abs = tile("gd_abs", [P, BLOCKS, PACK], F32)
         gd_floor = tile("gd_floor", [P, BLOCKS, PACK], F32)
@@ -125,7 +127,10 @@ def tile_list_cocoa_supply_tiers_kernel(
 
         def gather_table(a, halves):
             first, count = halves[0], len(halves)
-            picked = tile(f"v_codes{a}{first}", [P, count * BANK], U32)
+            if a == 1:
+                picked = shared.tile([P, BANK], U32, name=f"v_codes1{first}", offset=first * T, align_bytes=64)
+            else:
+                picked = tile(f"v_codes{a}{first}", [P, count * BANK], U32)
             nc.vector.tensor_copy(
                 picked[:], tab_w[a][:].indirect(offs_sb[:, first * BANK // 16 : (first + count) * BANK // 16])
             )
@@ -199,18 +204,29 @@ def tile_list_cocoa_supply_tiers_kernel(
                 in_=x_bf[:].rearrange("p m t -> p (m t)"),
             )
 
-        wp_codes = tile("wp_codes", [P, BLOCKS * 2 * H], U8)
+        wp_codes = {}
+
+        def deal_wp_words(b, first, count, tag):
+            dealt = tile(f"wp_codes{b}{first}", [P, BLOCKS, count * 2 * P], U8, tag=tag)
+            words = wp_raw[:].bitcast(U16).rearrange("p (a b m t) -> p b a t m", a=BLOCKS, b=BLOCKS, t=PACK)
+            nc.vector.tensor_copy(
+                dealt[:].bitcast(U16).rearrange("p a (t m) -> p a t m", t=count), words[:, b, :, first : first + count]
+            )
+            for i in range(count):
+                wp_codes[b, first + i] = dealt[:, :, i * 2 * P : (i + 1) * 2 * P]
+
         wp_sc = tile("wp_sc", [P, BLOCKS * H], U8)
         y = {}
 
-        def second_product(a):
-            for k, (b, t) in enumerate(SLICES):
+        def second_product(steps):
+            for k, a in steps:
+                b, t = SLICES[k]
                 if a == 0:
                     y[b, t] = psum.tile([P, BANK], F32, name=f"bank{k}")
                 c0 = a * H + b * KP + t * P
                 nc.tensor.matmul_mx(
                     out=y[b, t][:],
-                    lhsT=wp_codes[:, 2 * c0 : 2 * (c0 + P)].bitcast(FP4X4),
+                    lhsT=wp_codes[b, t][:, a, :].bitcast(FP4X4),
                     lhsT_scale=wp_sc[:, c0 : c0 + P],
                     rhs=x_codes[a][:].bitcast(FP8X4),
                     rhs_scale=x_scales[a][:],
@@ -221,34 +237,29 @@ def tile_list_cocoa_supply_tiers_kernel(
         by_half = [(t, half) for half in range(HALVES) for t in range(PACK)]
         by_slice = [(t, half) for t in range(PACK) for half in range(HALVES)]
 
+        opening = [(0, 0), (1, 0), (0, 1), (1, 1)] + by_slice[4:]
         gather_table(0, (0, 1))
         nc.vector.tensor_copy(v_scales[:], tab_sc[:].indirect(offs_sb[:]))
-        cast_w(0, 0, P)
-        quantize_w(0, 0)
+        for a in range(PASSES):
+            cast_w(0, a, P)
+            quantize_w(0, a)
         first_product(0, 0, by_half)
-        cast_w(0, 1, P)
-        quantize_w(0, 1)
-        gather_table(1, (0, 1))
-        first_product(0, 1, by_half)
-        nc.vector.tensor_copy(
-            wp_codes[:].bitcast(U16).rearrange("p (g t m) -> p g t m", t=PACK, m=P),
-            wp_raw[:].bitcast(U16).rearrange("p (g m t) -> p g t m", t=PACK, m=P),
-        )
         nc.vector.tensor_copy(
             wp_sc[:].rearrange("p (g t m) -> p g t m", t=PACK, m=P),
             wp_sc_raw[:].rearrange("p (g m t) -> p g t m", t=PACK, m=P),
         )
-        cast_w(0, 2, P)
-        quantize_w(0, 2)
+        for half in range(HALVES):
+            gather_table(1, (half,))
+        first_product(0, 1, by_half)
         gather_table(2, (0,))
         gather_table(2, (1,))
-        first_product(0, 2, by_half)
-        for t, half in by_half:
+        first_product(0, 2, opening)
+        for t, half in opening:
             empty_h(0, t, half)
         for a in range(2):
-            cast_w(1, a, 0)
+            cast_w(1, a, 0 if a else 0)
             quantize_w(1, a)
-            first_product(1, a, by_half)
+            first_product(1, a, opening)
         up_first = tile("up_first", [P, PACK, HALF_M], F32, tag="w_bf1")
         for t in range(PACK):
             gather_up(up_first[:, t, :], 0, t, 0, HALF_M)
@@ -271,7 +282,8 @@ def tile_list_cocoa_supply_tiers_kernel(
                     gather_up(up_last[:, t, m0 : m0 + HALF_M], 1, t, m0, HALF_M)
         x_second = round_x("x_second", up_second[:], "w_codes12")
         quantize_x(0, HALF_M, x_second)
-        second_product(0)
+        deal_wp_words(0, 0, EARLY, "w_bf2")
+        second_product([(k, 0) for k in range(EARLY)])
         down = {}
 
         def gather_down(name, ks, tag):
@@ -282,49 +294,68 @@ def tile_list_cocoa_supply_tiers_kernel(
 
         plain = list(range(FUSED, len(SLICES)))
         x_third = round_x("x_third", up_last[:, :, :HALF_M], "x_third")
-        x_fourth = round_x("x_fourth", up_last[:, :, HALF_M:], "x_fourth")
-        gather_down("down_early", plain[:1], "w_bf2")
+        x_fourth = round_x("x_fourth", up_last[:, :, HALF_M:], 0)
         quantize_x(1, 0, x_third)
         quantize_x(1, HALF_M, x_fourth)
-        second_product(1)
-        gather_down("down_late", plain[1:], "x_fourth")
-
-        def parts(k):
-            return [slice(0, HALF_M), slice(HALF_M, M)] if k == len(SLICES) - 1 else [slice(0, M)]
+        second_product([(k, 1) for k in range(EARLY)])
+        deal_wp_words(0, EARLY, PACK - EARLY, 0)
+        deal_wp_words(1, 0, PACK, "up_last")
+        second_product([(k, a) for k in range(EARLY, len(SLICES)) for a in range(BLOCKS)])
+        gather_down("down_late", plain, 1024)
 
         n = len(SLICES)
+        whole = slice(0, M)
+        halves = [slice(0, HALF_M), slice(HALF_M, M)]
         mag = {}
         roots = tile("roots", [P, n, M], F32, tag="tab_w0")
         damp = tile("damp", [P, n, M], F32, tag="tab_w1")
         res = tile("res", [P, n, M], F32, tag="tab_w2")
-        for step in range(n + 3):
-            if step < n:
-                mag[step] = ring.tile([P, M], F32, name="mag")
-                nc.scalar.activation(mag[step][:], y[SLICES[step]][:], ACT.Abs)
-            k = step - 1
-            if 0 <= k < n:
-                nc.scalar.activation(roots[:, k, :], mag[k][:], ACT.Abs_reciprocal_sqrt, bias=1.0)
-            k = step - 2
-            if 0 <= k < n:
-                b, t = SLICES[k]
-                if k in SQUARED_ON_VECTOR:
-                    nc.vector.scalar_tensor_tensor(
-                        damp[:, k, :], roots[:, k, :], gd_abs[:, b, t : t + 1], roots[:, k, :], ALU.mult, ALU.mult
-                    )
-                else:
-                    for cols in parts(k):
-                        nc.scalar.activation(
-                            damp[:, k, cols], roots[:, k, cols], ACT.Square, scale=gd_root[:, b, t : t + 1]
-                        )
-            k = step - 3
-            if 0 <= k:
-                b, t = SLICES[k]
-                for cols in parts(k):
-                    if k < FUSED:
-                        nc.vector.tensor_tensor(res[:, k, :], h[b, t][:].indirect(pos2_sb[:]), damp[:, k, :], ALU.mult)
-                    else:
-                        nc.vector.tensor_tensor(res[:, k, cols], damp[:, k, cols], down[k][:, cols], ALU.mult)
-                    nc.sync.dma_start(
-                        out=out[b * KP : (b + 1) * KP, :].rearrange("(p t) m -> p t m", t=PACK)[:, t, cols],
-                        in_=res[:, k, cols],
-                    )
+
+        def magnitude(k, cols):
+            if k not in mag:
+                mag[k] = ring.tile([P, M], F32, name="mag")
+            nc.scalar.activation(mag[k][:, cols], y[SLICES[k]][:, cols], ACT.Abs)
+
+        def root(k, cols):
+            nc.scalar.activation(roots[:, k, cols], mag[k][:, cols], ACT.Abs_reciprocal_sqrt, bias=1.0)
+
+        def square(k, cols):
+            b, t = SLICES[k]
+            if k < SQUARED_ON_VECTOR:
+                nc.vector.scalar_tensor_tensor(
+                    damp[:, k, cols], roots[:, k, cols], gd_abs[:, b, t : t + 1], roots[:, k, cols], ALU.mult, ALU.mult
+                )
+            else:
+                nc.scalar.activation(damp[:, k, cols], roots[:, k, cols], ACT.Square, scale=gd_root[:, b, t : t + 1])
+
+        def finish(k, cols):
+            b, t = SLICES[k]
+            if k < FUSED:
+                nc.vector.tensor_tensor(res[:, k, :], h[b, t][:].indirect(pos2_sb[:]), damp[:, k, :], ALU.mult)
+            else:
+                nc.vector.tensor_tensor(res[:, k, cols], damp[:, k, cols], down[k][:, cols], ALU.mult)
+            nc.sync.dma_start(
+                out=out[b * KP : (b + 1) * KP, :].rearrange("(p t) m -> p t m", t=PACK)[:, t, cols],
+                in_=res[:, k, cols],
+            )
+
+        magnitude(0, whole)
+        magnitude(1, whole)
+        root(0, whole)
+        magnitude(2, whole)
+        square(0, whole)
+        root(1, whole)
+        finish(0, whole)
+        square(1, whole)
+        finish(1, whole)
+        for k in range(2, n - 1):
+            root(k, whole)
+            magnitude(k + 1, whole if k + 1 < n - 1 else halves[0])
+            square(k, whole)
+            finish(k, whole)
+        magnitude(n - 1, halves[1])
+        for cols in halves:
+            root(n - 1, cols)
+        for cols in halves:
+            square(n - 1, cols)
+            finish(n - 1, cols)

@@ -137,23 +137,31 @@ def tile_list_cocoa_supply_tiers_kernel(
             for i, half in enumerate(halves):
                 v_codes[a, half] = picked[:, i * BANK : (i + 1) * BANK]
 
-        def cast_w(b, a, on_scalar):
-            w_bf[b, a] = tile(f"w_bf{b}{a}", [P, PACK, P, PACK], BF16, tag=f"w_bf{a}")
-            dst = w_bf[b, a][:].rearrange("p t m j -> p m j t")
-            src = w_raw[b, a][:].rearrange("p j (m t) -> p m j t", t=PACK)
-            if on_scalar > 0:
-                nc.scalar.activation(dst[:, :on_scalar], src[:, :on_scalar], ACT.Copy)
-            if on_scalar < P:
-                nc.vector.tensor_copy(dst[:, on_scalar:], src[:, on_scalar:])
+        def cast_w(b, a, first, count, engine, tag):
+            w_bf[b, a, first] = tile(f"w_bf{b}{a}{first}", [P, count, P, PACK], BF16, tag=tag)
+            dst = w_bf[b, a, first][:].rearrange("p t m j -> p m j t")
+            src = w_raw[b, a][:].rearrange("p j (m t) -> p m j t", t=PACK)[:, :, :, first : first + count]
+            if engine == "scalar":
+                nc.scalar.activation(dst, src, ACT.Copy)
+            elif engine == "vector":
+                nc.vector.tensor_copy(dst, src)
+            else:
+                dst = dst.rearrange("p m j t -> p m t j")
+                src = src.rearrange("p m j t -> p m t j")
+                nc.gpsimd.tensor_scalar(dst, src, 1.0, 0.0, ALU.mult, ALU.add)
 
-        def quantize_w(b, a):
-            w_codes[b, a] = tile(f"w_codes{b}{a}", [P, KP], U32)
-            w_scales[b, a] = tile(f"w_scales{b}{a}", [P, KP], U8)
+        def quantize_w(b, a, first, tag=None):
+            count = w_bf[b, a, first].shape[1]
+            codes = tile(f"w_codes{b}{a}{first}", [P, count * P], U32, tag=tag)
+            scales = tile(f"w_scales{b}{a}{first}", [P, count * P], U8)
             nc.vector.quantize_mx(
-                out=w_codes[b, a][:].bitcast(FP8X4),
-                scales=w_scales[b, a][:],
-                in_=w_bf[b, a][:].rearrange("p t m j -> p (t m j)"),
+                out=codes[:].bitcast(FP8X4),
+                scales=scales[:],
+                in_=w_bf[b, a, first][:].rearrange("p t m j -> p (t m j)"),
             )
+            for i in range(count):
+                w_codes[b, a, first + i] = codes[:, i * P : (i + 1) * P]
+                w_scales[b, a, first + i] = scales[:, i * P : (i + 1) * P]
 
         banks = {}
 
@@ -163,8 +171,8 @@ def tile_list_cocoa_supply_tiers_kernel(
                     banks[b, t, half] = psum.tile([P, BANK], F32, name=f"bank{HALVES * t + half}")
                 nc.tensor.matmul_mx(
                     out=banks[b, t, half][:],
-                    lhsT=w_codes[b, a][:, t * P : (t + 1) * P].bitcast(FP8X4),
-                    lhsT_scale=w_scales[b, a][:, t * P : (t + 1) * P],
+                    lhsT=w_codes[b, a, t].bitcast(FP8X4),
+                    lhsT_scale=w_scales[b, a, t],
                     rhs=v_codes[a, half].bitcast(FP8X4),
                     rhs_scale=v_scales[4 * a : P, half * BANK : (half + 1) * BANK],
                     start=(a == 0),
@@ -241,8 +249,8 @@ def tile_list_cocoa_supply_tiers_kernel(
         gather_table(0, (0, 1))
         nc.vector.tensor_copy(v_scales[:], tab_sc[:].indirect(offs_sb[:]))
         for a in range(PASSES):
-            cast_w(0, a, P)
-            quantize_w(0, a)
+            cast_w(0, a, 0, PACK, "scalar", f"w_bf{a}")
+            quantize_w(0, a, 0)
         first_product(0, 0, by_half)
         nc.vector.tensor_copy(
             wp_sc[:].rearrange("p (g t m) -> p g t m", t=PACK, m=P),
@@ -256,18 +264,23 @@ def tile_list_cocoa_supply_tiers_kernel(
         first_product(0, 2, opening)
         for t, half in opening:
             empty_h(0, t, half)
-        for a in range(2):
-            cast_w(1, a, 0 if a else 0)
-            quantize_w(1, a)
-            first_product(1, a, opening)
-        up_first = tile("up_first", [P, PACK, HALF_M], F32, tag="w_bf1")
+        cast_w(1, 0, 0, PACK, "vector", "w_bf0")
+        quantize_w(1, 0, 0)
+        first_product(1, 0, opening)
+        cast_w(1, 1, 0, PACK, "gpsimd", "w_bf1")
+        up_first = tile("up_first", [P, PACK, HALF_M], F32, tag="w_bf0")
         for t in range(PACK):
             gather_up(up_first[:, t, :], 0, t, 0, HALF_M)
-        cast_w(1, 2, P)
-        quantize_w(1, 2)
-        first_product(1, 2, by_slice)
+        cast_w(1, 2, 0, 2, "scalar", "w_bf_pair0")
+        cast_w(1, 2, 2, 2, "vector", "w_bf_pair2")
+        quantize_w(1, 1, 0)
+        quantize_w(1, 2, 0, tag="w_bf1")
+        quantize_w(1, 2, 2, tag="w_bf_pair0")
+        for bank in by_slice:
+            for a in (1, 2):
+                first_product(1, a, [bank])
         x_first = round_x("x_first", up_first[:], "w_raw12")
-        up_second = tile("up_second", [P, PACK, HALF_M], F32, tag="w_bf2")
+        up_second = tile("up_second", [P, PACK, HALF_M], F32, tag="w_bf_pair2")
         for t in range(PACK):
             gather_up(up_second[:, t, :], 0, t, HALF_M, HALF_M)
         quantize_x(0, 0, x_first)
@@ -280,9 +293,9 @@ def tile_list_cocoa_supply_tiers_kernel(
             else:
                 for m0 in (0, HALF_M):
                     gather_up(up_last[:, t, m0 : m0 + HALF_M], 1, t, m0, HALF_M)
-        x_second = round_x("x_second", up_second[:], "w_codes12")
+        x_second = round_x("x_second", up_second[:], "w_bf_pair0")
         quantize_x(0, HALF_M, x_second)
-        deal_wp_words(0, 0, EARLY, "w_bf2")
+        deal_wp_words(0, 0, EARLY, "w_bf_pair2")
         second_product([(k, 0) for k in range(EARLY)])
         down = {}
 

@@ -26,6 +26,7 @@ HALVES = S // BANK
 HALF_M = M // 2
 SLICES = [(b, t) for b in range(BLOCKS) for t in range(PACK)]
 EARLY = 2
+LAST_RUNS = ((0, 128), (128, 128), (256, 256))
 SMALLEST_NORMAL = 2.0**-126
 FUSED = 7
 SQUARED_ON_VECTOR = 2
@@ -55,8 +56,8 @@ def tile_list_cocoa_supply_tiers_kernel(
         wp_sc_raw = shared.tile([P, BLOCKS * H], U8, name="wp_sc_raw", offset=T, align_bytes=64)
         nc.vector.memset(wp_sc_raw[:].bitcast(I32), 0)
         nc.vector.memset(tab_sc[:].bitcast(I32), 0)
-        b1_sb = tile("b1_sb", [P, BLOCKS, PACK], F32)
-        gd_sb = tile("gd_sb", [P, BLOCKS, PACK], F32)
+        b1_sb = tile("b1_sb", [P, BLOCKS, 2 * PACK], F32)[:, :, :PACK]
+        gd_sb = tile("gd_sb", [P, BLOCKS, 2 * PACK], F32)[:, :, :PACK]
         tab_w = [tile(f"tab_w{a}", [P, T], U32) for a in range(PASSES)]
         w_raw = {(b, a): tile(f"w_raw{b}{a}", [P, PACK, KP], F32) for b in range(BLOCKS) for a in range(PASSES)}
         wp_raw = tile("wp_raw", [P, BLOCKS * 2 * H], U8)
@@ -86,16 +87,15 @@ def tile_list_cocoa_supply_tiers_kernel(
                 out=tab_sc[32 * q : 32 * q + 4 * PASSES, :].bitcast(I32),
                 in_=tab_scales[:, 4 * q : 4 * q + 4, :].bitcast(I32),
             )
-        nc.sync.dma_start(out=gd_sb[:], in_=gd.rearrange("(b p t) -> p b t", p=P, t=PACK))
+        nc.sync.dma_start(out=gd_sb, in_=gd.rearrange("(b p t) -> p b t", p=P, t=PACK))
         for a in range(PASSES):
             load_w(0, a)
-        nc.sync.dma_start(out=b1_sb[:], in_=b1.rearrange("(b p t) -> p b t", p=P, t=PACK))
+        nc.sync.dma_start(out=b1_sb, in_=b1.rearrange("(b p t) -> p b t", p=P, t=PACK))
         nc.sync.dma_start(pos1_sb[:], pos1)
         for q in range(3):
             load_wp_scales(q)
         load_table(1)
         load_wp_scales(3)
-        nc.sync.dma_start(pos2_sb[:], pos2)
         load_table(2)
         for a in range(PASSES):
             load_w(1, a)
@@ -103,6 +103,7 @@ def tile_list_cocoa_supply_tiers_kernel(
             out=wp_raw[:].bitcast(I32).rearrange("p (a c) -> p a c", a=BLOCKS),
             in_=wp_words.bitcast(I32).rearrange("a p c -> p a c"),
         )
+        nc.sync.dma_start(pos2_sb[:], pos2)
 
         gd_abs = tile("gd_abs", [P, BLOCKS, PACK], F32)
         gd_floor = tile("gd_floor", [P, BLOCKS, PACK], F32)
@@ -111,10 +112,10 @@ def tile_list_cocoa_supply_tiers_kernel(
         positive = tile("positive", [P, BLOCKS, PACK], F32)
         sign = tile("sign", [P, BLOCKS, PACK], F32)
         b1_signed = tile("b1_signed", [P, BLOCKS, PACK], F32)
-        nc.vector.tensor_scalar(positive[:], gd_sb[:], 0.0, None, ALU.is_ge)
+        nc.vector.tensor_scalar(positive[:], gd_sb, 0.0, None, ALU.is_ge)
         nc.vector.tensor_scalar(sign[:], positive[:], 2.0, -1.0, ALU.mult, ALU.add)
-        nc.vector.tensor_tensor(gd_abs[:], gd_sb[:], sign[:], ALU.mult)
-        nc.vector.tensor_tensor(b1_signed[:], b1_sb[:], sign[:], ALU.mult)
+        nc.vector.tensor_tensor(gd_abs[:], gd_sb, sign[:], ALU.mult)
+        nc.vector.tensor_tensor(b1_signed[:], b1_sb, sign[:], ALU.mult)
         nc.vector.tensor_scalar(gd_floor[:], gd_abs[:], SMALLEST_NORMAL, None, ALU.max)
         nc.scalar.activation(gd_rsqrt[:], gd_floor[:], ACT.Abs_reciprocal_sqrt)
         nc.vector.tensor_tensor(gd_root[:], gd_abs[:], gd_rsqrt[:], ALU.mult)
@@ -150,9 +151,9 @@ def tile_list_cocoa_supply_tiers_kernel(
                 src = src.rearrange("p m j t -> p m t j")
                 nc.gpsimd.tensor_scalar(dst, src, 1.0, 0.0, ALU.mult, ALU.add)
 
-        def quantize_w(b, a, first, tag=None):
+        def quantize_w(b, a, first):
             count = w_bf[b, a, first].shape[1]
-            codes = tile(f"w_codes{b}{a}{first}", [P, count * P], U32, tag=tag)
+            codes = tile(f"w_codes{b}{a}{first}", [P, count * P], U32)
             scales = tile(f"w_scales{b}{a}{first}", [P, count * P], U8)
             nc.vector.quantize_mx(
                 out=codes[:].bitcast(FP8X4),
@@ -190,19 +191,21 @@ def tile_list_cocoa_supply_tiers_kernel(
                 scale=sign[:, b, t : t + 1],
             )
 
-        x_codes = [tile(f"x_codes{b}", [P, M], U32) for b in range(BLOCKS)]
+        x_codes = {1: tile("x_codes1", [P, M], U32)}
         x_scales = [tile(f"x_scales{b}", [P, M], U8) for b in range(BLOCKS)]
 
         def gather_up(dst, b, t, m0, width):
             nc.vector.tensor_copy(dst, h[b, t][:].indirect(pos1_sb[:, m0 // 16 : (m0 + width) // 16]))
 
-        def round_x(name, up, tag):
+        def round_x(name, up, tag, pieces=1):
             x_bf = tile(name, [P, HALF_M, PACK], BF16, tag=tag)
-            nc.scalar.activation(
-                x_bf[:].rearrange("p (c i) t -> p c t i", i=4),
-                up.rearrange("p t (c i) -> p c t i", i=4),
-                ACT.Abs,
-            )
+            for i in range(pieces):
+                cols = slice(i * HALF_M // pieces, (i + 1) * HALF_M // pieces)
+                nc.scalar.activation(
+                    x_bf[:, cols].rearrange("p (c i) t -> p c t i", i=4),
+                    up[:, :, cols].rearrange("p t (c i) -> p c t i", i=4),
+                    ACT.Abs,
+                )
             return x_bf
 
         def quantize_x(b, m0, x_bf):
@@ -271,19 +274,18 @@ def tile_list_cocoa_supply_tiers_kernel(
         up_first = tile("up_first", [P, PACK, HALF_M], F32, tag="w_bf0")
         for t in range(PACK):
             gather_up(up_first[:, t, :], 0, t, 0, HALF_M)
-        cast_w(1, 2, 0, 2, "scalar", "w_bf_pair0")
-        cast_w(1, 2, 2, 2, "vector", "w_bf_pair2")
         quantize_w(1, 1, 0)
-        quantize_w(1, 2, 0, tag="w_bf1")
-        quantize_w(1, 2, 2, tag="w_bf_pair0")
+        cast_w(1, 2, 0, 2, "scalar", 8320)
+        quantize_w(1, 2, 0)
+        cast_w(1, 2, 2, 2, "gpsimd", 10304)
+        quantize_w(1, 2, 2)
         for bank in by_slice:
             for a in (1, 2):
                 first_product(1, a, [bank])
-        x_first = round_x("x_first", up_first[:], "w_raw12")
-        up_second = tile("up_second", [P, PACK, HALF_M], F32, tag="w_bf_pair2")
+        x_first = round_x("x_first", up_first[:], "w_bf1")
+        up_second = tile("up_second", [P, PACK, HALF_M], F32, tag=6208)
         for t in range(PACK):
             gather_up(up_second[:, t, :], 0, t, HALF_M, HALF_M)
-        quantize_x(0, 0, x_first)
         up_last = tile("up_last", [P, PACK, M], F32)
         for t in range(PACK):
             for half in range(HALVES):
@@ -291,11 +293,13 @@ def tile_list_cocoa_supply_tiers_kernel(
             if t < PACK - 1:
                 gather_up(up_last[:, t, :], 1, t, 0, M)
             else:
-                for m0 in (0, HALF_M):
-                    gather_up(up_last[:, t, m0 : m0 + HALF_M], 1, t, m0, HALF_M)
-        x_second = round_x("x_second", up_second[:], "w_bf_pair0")
+                for m0, width in LAST_RUNS:
+                    gather_up(up_last[:, t, m0 : m0 + width], 1, t, m0, width)
+        x_second = round_x("x_second", up_second[:], "w_codes122")
+        x_codes[0] = tile("x_codes0", [P, M], U32, tag=7232)
+        quantize_x(0, 0, x_first)
         quantize_x(0, HALF_M, x_second)
-        deal_wp_words(0, 0, EARLY, "w_bf_pair2")
+        deal_wp_words(0, 0, EARLY, 6208)
         second_product([(k, 0) for k in range(EARLY)])
         down = {}
 
@@ -306,15 +310,15 @@ def tile_list_cocoa_supply_tiers_kernel(
                 nc.vector.tensor_copy(down[k], h[SLICES[k]][:].indirect(pos2_sb[:]))
 
         plain = list(range(FUSED, len(SLICES)))
-        x_third = round_x("x_third", up_last[:, :, :HALF_M], "x_third")
-        x_fourth = round_x("x_fourth", up_last[:, :, HALF_M:], 0)
+        x_third = round_x("x_third", up_last[:, :, :HALF_M], "x_third", pieces=2)
+        x_fourth = round_x("x_fourth", up_last[:, :, HALF_M:], 2048)
         quantize_x(1, 0, x_third)
         quantize_x(1, HALF_M, x_fourth)
         second_product([(k, 1) for k in range(EARLY)])
-        deal_wp_words(0, EARLY, PACK - EARLY, 0)
-        deal_wp_words(1, 0, PACK, "up_last")
+        deal_wp_words(0, EARLY, PACK - EARLY, 2112)
+        deal_wp_words(1, 0, PACK, 64)
         second_product([(k, a) for k in range(EARLY, len(SLICES)) for a in range(BLOCKS)])
-        gather_down("down_late", plain, 1024)
+        gather_down("down_late", plain, 3136)
 
         n = len(SLICES)
         whole = slice(0, M)

@@ -29,7 +29,7 @@ EARLY = 2
 LAST_RUNS = ((0, 128), (128, 128), (256, 256))
 SMALLEST_NORMAL = 2.0**-126
 FUSED = 7
-SQUARED_ON_VECTOR = 2
+SQUARED_ON_VECTOR = 3
 
 
 def tile_list_cocoa_supply_tiers_kernel(
@@ -138,18 +138,22 @@ def tile_list_cocoa_supply_tiers_kernel(
             for i, half in enumerate(halves):
                 v_codes[a, half] = picked[:, i * BANK : (i + 1) * BANK]
 
-        def cast_w(b, a, first, count, engine, tag):
-            w_bf[b, a, first] = tile(f"w_bf{b}{a}{first}", [P, count, P, PACK], BF16, tag=tag)
-            dst = w_bf[b, a, first][:].rearrange("p t m j -> p m j t")
-            src = w_raw[b, a][:].rearrange("p j (m t) -> p m j t", t=PACK)[:, :, :, first : first + count]
-            if engine == "scalar":
-                nc.scalar.activation(dst, src, ACT.Copy)
-            elif engine == "vector":
-                nc.vector.tensor_copy(dst, src)
-            else:
-                dst = dst.rearrange("p m j t -> p m t j")
-                src = src.rearrange("p m j t -> p m t j")
-                nc.gpsimd.tensor_scalar(dst, src, 1.0, 0.0, ALU.mult, ALU.add)
+        def cast_w(b, a, first, count, engines, tag):
+            w_bf[b, a, first] = tile(f"w_bf{b}{a}{first}", [P, PACK, P, PACK], BF16, tag=tag)[:, :count]
+            share = count // len(engines)
+            for i, engine in enumerate(engines):
+                t0 = i * share
+                dst = w_bf[b, a, first][:, t0 : t0 + share].rearrange("p t m j -> p m j t")
+                src = w_raw[b, a][:].rearrange("p j (m t) -> p m j t", t=PACK)
+                src = src[:, :, :, first + t0 : first + t0 + share]
+                if engine == "scalar":
+                    nc.scalar.activation(dst, src, ACT.Copy)
+                elif engine == "vector":
+                    nc.vector.tensor_copy(dst, src)
+                else:
+                    dst = dst.rearrange("p m j t -> p m t j")
+                    src = src.rearrange("p m j t -> p m t j")
+                    nc.gpsimd.tensor_scalar(dst, src, 1.0, 0.0, ALU.mult, ALU.add)
 
         def quantize_w(b, a, first):
             count = w_bf[b, a, first].shape[1]
@@ -158,7 +162,7 @@ def tile_list_cocoa_supply_tiers_kernel(
             nc.vector.quantize_mx(
                 out=codes[:].bitcast(FP8X4),
                 scales=scales[:],
-                in_=w_bf[b, a, first][:].rearrange("p t m j -> p (t m j)"),
+                in_=w_bf[b, a, first].rearrange("p t m j -> p (t m j)"),
             )
             for i in range(count):
                 w_codes[b, a, first + i] = codes[:, i * P : (i + 1) * P]
@@ -252,7 +256,7 @@ def tile_list_cocoa_supply_tiers_kernel(
         gather_table(0, (0, 1))
         nc.vector.tensor_copy(v_scales[:], tab_sc[:].indirect(offs_sb[:]))
         for a in range(PASSES):
-            cast_w(0, a, 0, PACK, "scalar", f"w_bf{a}")
+            cast_w(0, a, 0, PACK, ["scalar"], f"w_bf{a}")
             quantize_w(0, a, 0)
         first_product(0, 0, by_half)
         nc.vector.tensor_copy(
@@ -267,22 +271,24 @@ def tile_list_cocoa_supply_tiers_kernel(
         first_product(0, 2, opening)
         for t, half in opening:
             empty_h(0, t, half)
-        cast_w(1, 0, 0, PACK, "vector", "w_bf0")
+        cast_w(1, 0, 0, PACK, ["vector"], "w_bf0")
         quantize_w(1, 0, 0)
         first_product(1, 0, opening)
-        cast_w(1, 1, 0, PACK, "gpsimd", "w_bf1")
-        up_first = tile("up_first", [P, PACK, HALF_M], F32, tag="w_bf0")
+        cast_w(1, 1, 0, 2, ["vector"], 16448)
+        quantize_w(1, 1, 0)
+        cast_w(1, 1, 2, 2, ["gpsimd"], 12416)
+        up_first = tile("up_first", [P, PACK, HALF_M], F32, tag=20480)
         for t in range(PACK):
             gather_up(up_first[:, t, :], 0, t, 0, HALF_M)
-        quantize_w(1, 1, 0)
-        cast_w(1, 2, 0, 2, "scalar", 8320)
+        cast_w(1, 2, 0, 2, ["scalar"], 8320)
         quantize_w(1, 2, 0)
-        cast_w(1, 2, 2, 2, "gpsimd", 10304)
+        quantize_w(1, 1, 2)
+        cast_w(1, 2, 2, 2, ["gpsimd"], 12352)
         quantize_w(1, 2, 2)
         for bank in by_slice:
             for a in (1, 2):
                 first_product(1, a, [bank])
-        x_first = round_x("x_first", up_first[:], "w_bf1")
+        x_first = round_x("x_first", up_first[:], 10304)
         up_second = tile("up_second", [P, PACK, HALF_M], F32, tag=6208)
         for t in range(PACK):
             gather_up(up_second[:, t, :], 0, t, HALF_M, HALF_M)

@@ -25,10 +25,10 @@ BLOCKS = H // KP
 HALVES = S // BANK
 HALF_M = M // 2
 SLICES = [(b, t) for b in range(BLOCKS) for t in range(PACK)]
-EARLY = 2
+UNITS = [(0, (0, 1), slice(m0, m0 + HALF_M)) for m0 in (0, HALF_M)]
+UNITS = UNITS + [(b, (t,), slice(0, M)) for b, t in SLICES[2:]]
 LAST_RUNS = ((0, 128), (128, 128), (256, 256))
 SMALLEST_NORMAL = 2.0**-126
-FUSED = 7
 SQUARED_ON_VECTOR = 3
 
 
@@ -233,20 +233,24 @@ def tile_list_cocoa_supply_tiers_kernel(
         wp_sc = tile("wp_sc", [P, BLOCKS * H], U8)
         y = {}
 
-        def second_product(steps):
-            for k, a in steps:
-                b, t = SLICES[k]
-                if a == 0:
-                    y[b, t] = psum.tile([P, BANK], F32, name=f"bank{k}")
+        def second_product(u, a):
+            b, ts, entries = UNITS[u]
+            if a == 0:
+                y[u] = psum.tile([P, BANK], F32, name=f"bank{u}")
+            width = BANK if len(ts) == 1 else P
+            count = BANK // width
+            for i in range(count):
+                t = ts[i * len(ts) // count]
+                m0 = entries.start + i % 2 * width
                 c0 = a * H + b * KP + t * P
                 nc.tensor.matmul_mx(
-                    out=y[b, t][:],
+                    out=y[u][:, i * width : (i + 1) * width],
                     lhsT=wp_codes[b, t][:, a, :].bitcast(FP4X4),
                     lhsT_scale=wp_sc[:, c0 : c0 + P],
-                    rhs=x_codes[a][:].bitcast(FP8X4),
-                    rhs_scale=x_scales[a][:],
-                    start=(a == 0),
-                    stop=(a == BLOCKS - 1),
+                    rhs=x_codes[a][:, m0 : m0 + width].bitcast(FP8X4),
+                    rhs_scale=x_scales[a][:, m0 : m0 + width],
+                    start=(a, i) == (0, 0),
+                    stop=(a, i) == (BLOCKS - 1, count - 1),
                 )
 
         by_half = [(t, half) for half in range(HALVES) for t in range(PACK)]
@@ -304,29 +308,25 @@ def tile_list_cocoa_supply_tiers_kernel(
         x_second = round_x("x_second", up_second[:], "w_codes122")
         x_codes[0] = tile("x_codes0", [P, M], U32, tag=7232)
         quantize_x(0, 0, x_first)
-        quantize_x(0, HALF_M, x_second)
-        deal_wp_words(0, 0, EARLY, 6208)
-        second_product([(k, 0) for k in range(EARLY)])
-        down = {}
-
-        def gather_down(name, ks, tag):
-            picked = tile(name, [P, len(ks), M], F32, tag=tag)
-            for i, k in enumerate(ks):
-                down[k] = picked[:, i, :]
-                nc.vector.tensor_copy(down[k], h[SLICES[k]][:].indirect(pos2_sb[:]))
-
-        plain = list(range(FUSED, len(SLICES)))
+        deal_wp_words(0, 0, 2, 6208)
+        second_product(0, 0)
         x_third = round_x("x_third", up_last[:, :, :HALF_M], "x_third", pieces=2)
-        x_fourth = round_x("x_fourth", up_last[:, :, HALF_M:], 2048)
         quantize_x(1, 0, x_third)
+        second_product(0, 1)
+        quantize_x(0, HALF_M, x_second)
+        second_product(1, 0)
+        x_fourth = round_x("x_fourth", up_last[:, :, HALF_M:], 2048)
         quantize_x(1, HALF_M, x_fourth)
-        second_product([(k, 1) for k in range(EARLY)])
-        deal_wp_words(0, EARLY, PACK - EARLY, 2112)
+        second_product(1, 1)
+        deal_wp_words(0, 2, 2, 2112)
         deal_wp_words(1, 0, PACK, 64)
-        second_product([(k, a) for k in range(EARLY, len(SLICES)) for a in range(BLOCKS)])
-        gather_down("down_late", plain, 3136)
+        for u in range(2, len(UNITS)):
+            for a in range(BLOCKS):
+                second_product(u, a)
+        down = tile("down", [P, M], F32, tag=3136)
+        nc.vector.tensor_copy(down[:], h[SLICES[-1]][:].indirect(pos2_sb[:]))
 
-        n = len(SLICES)
+        n = len(UNITS)
         whole = slice(0, M)
         halves = [slice(0, HALF_M), slice(HALF_M, M)]
         mag = {}
@@ -334,48 +334,48 @@ def tile_list_cocoa_supply_tiers_kernel(
         damp = tile("damp", [P, n, M], F32, tag="tab_w1")
         res = tile("res", [P, n, M], F32, tag="tab_w2")
 
-        def magnitude(k, cols):
-            if k not in mag:
-                mag[k] = ring.tile([P, M], F32, name="mag")
-            nc.scalar.activation(mag[k][:, cols], y[SLICES[k]][:, cols], ACT.Abs)
+        def runs(u, cols):
+            ts = UNITS[u][1]
+            return [(ts[0], cols)] if len(ts) == 1 else list(zip(ts, halves))
 
-        def root(k, cols):
-            nc.scalar.activation(roots[:, k, cols], mag[k][:, cols], ACT.Abs_reciprocal_sqrt, bias=1.0)
+        def magnitude(u, cols):
+            if u not in mag:
+                mag[u] = ring.tile([P, M], F32, name="mag")
+            nc.scalar.activation(mag[u][:, cols], y[u][:, cols], ACT.Abs)
 
-        def square(k, cols):
-            b, t = SLICES[k]
-            if k < SQUARED_ON_VECTOR:
-                nc.vector.scalar_tensor_tensor(
-                    damp[:, k, cols], roots[:, k, cols], gd_abs[:, b, t : t + 1], roots[:, k, cols], ALU.mult, ALU.mult
-                )
-            else:
-                nc.scalar.activation(damp[:, k, cols], roots[:, k, cols], ACT.Square, scale=gd_root[:, b, t : t + 1])
+        def root(u, cols):
+            nc.scalar.activation(roots[:, u, cols], mag[u][:, cols], ACT.Abs_reciprocal_sqrt, bias=1.0)
 
-        def finish(k, cols):
-            b, t = SLICES[k]
-            if k < FUSED:
-                nc.vector.tensor_tensor(res[:, k, :], h[b, t][:].indirect(pos2_sb[:]), damp[:, k, :], ALU.mult)
-            else:
-                nc.vector.tensor_tensor(res[:, k, cols], damp[:, k, cols], down[k][:, cols], ALU.mult)
+        def square(u, cols):
+            b = UNITS[u][0]
+            for t, run in runs(u, cols):
+                if u < SQUARED_ON_VECTOR:
+                    nc.vector.scalar_tensor_tensor(
+                        damp[:, u, run], roots[:, u, run], gd_abs[:, b, t : t + 1], roots[:, u, run], ALU.mult, ALU.mult
+                    )
+                else:
+                    nc.scalar.activation(damp[:, u, run], roots[:, u, run], ACT.Square, scale=gd_root[:, b, t : t + 1])
+
+        def finish(u, cols):
+            b, ts, entries = UNITS[u]
+            rows = out[b * KP : (b + 1) * KP, :].rearrange("(p t) m -> p t m", t=PACK)
+            if u == n - 1:
+                nc.vector.tensor_tensor(res[:, u, cols], damp[:, u, cols], down[:, cols], ALU.mult)
+                nc.sync.dma_start(out=rows[:, ts[0], cols], in_=res[:, u, cols])
+                return
+            offsets = pos2_sb[:, entries.start // 16 : entries.stop // 16]
+            for t, run in runs(u, cols):
+                nc.vector.tensor_tensor(res[:, u, run], h[b, t][:].indirect(offsets), damp[:, u, run], ALU.mult)
             nc.sync.dma_start(
-                out=out[b * KP : (b + 1) * KP, :].rearrange("(p t) m -> p t m", t=PACK)[:, t, cols],
-                in_=res[:, k, cols],
+                out=rows[:, ts[0] : ts[-1] + 1, entries], in_=res[:, u, :].rearrange("p (t m) -> p t m", t=len(ts))
             )
 
         magnitude(0, whole)
-        magnitude(1, whole)
-        root(0, whole)
-        magnitude(2, whole)
-        square(0, whole)
-        root(1, whole)
-        finish(0, whole)
-        square(1, whole)
-        finish(1, whole)
-        for k in range(2, n - 1):
-            root(k, whole)
-            magnitude(k + 1, whole if k + 1 < n - 1 else halves[0])
-            square(k, whole)
-            finish(k, whole)
+        for u in range(n - 1):
+            root(u, whole)
+            magnitude(u + 1, whole if u + 1 < n - 1 else halves[0])
+            square(u, whole)
+            finish(u, whole)
         magnitude(n - 1, halves[1])
         for cols in halves:
             root(n - 1, cols)

@@ -84,7 +84,7 @@ def tile_list_cocoa_supply_tiers_kernel(
         load_table(0)
         for q in range(4):
             nc.gpsimd.dma_start(
-                out=tab_sc[32 * q : 32 * q + 4 * PASSES, :].bitcast(I32),
+                out=tab_sc[32 * q + 4 : 32 * q + 4 + 4 * PASSES, :].bitcast(I32),
                 in_=tab_scales[:, 4 * q : 4 * q + 4, :].bitcast(I32),
             )
         nc.sync.dma_start(out=gd_sb, in_=gd.rearrange("(b p t) -> p b t", p=P, t=PACK))
@@ -179,7 +179,7 @@ def tile_list_cocoa_supply_tiers_kernel(
                     lhsT=w_codes[b, a, t].bitcast(FP8X4),
                     lhsT_scale=w_scales[b, a, t],
                     rhs=v_codes[a, half].bitcast(FP8X4),
-                    rhs_scale=v_scales[4 * a : P, half * BANK : (half + 1) * BANK],
+                    rhs_scale=v_scales[4 * (a + 1) : P, half * BANK : (half + 1) * BANK],
                     start=(a == 0),
                     stop=(a == PASSES - 1),
                 )

@@ -87,15 +87,14 @@ def tile_list_cocoa_supply_tiers_kernel(
                 out=tab_sc[32 * q + 4 : 32 * q + 4 + 4 * PASSES, :].bitcast(I32),
                 in_=tab_scales[:, 4 * q : 4 * q + 4, :].bitcast(I32),
             )
-        nc.sync.dma_start(out=gd_sb, in_=gd.rearrange("(b p t) -> p b t", p=P, t=PACK))
+        nc.scalar.dma_start(out=gd_sb, in_=gd.rearrange("(b p t) -> p b t", p=P, t=PACK))
         for a in range(PASSES):
             load_w(0, a)
-        nc.sync.dma_start(out=b1_sb, in_=b1.rearrange("(b p t) -> p b t", p=P, t=PACK))
+        nc.scalar.dma_start(out=b1_sb, in_=b1.rearrange("(b p t) -> p b t", p=P, t=PACK))
         nc.sync.dma_start(pos1_sb[:], pos1)
-        for q in range(3):
+        for q in range(4):
             load_wp_scales(q)
         load_table(1)
-        load_wp_scales(3)
         load_table(2)
         for a in range(PASSES):
             load_w(1, a)

@@ -54,8 +54,8 @@ def tile_list_cocoa_supply_tiers_kernel(
 
         tab_sc = shared.tile([P, T], U8, name="tab_sc", offset=0, align_bytes=64)
         wp_sc_raw = shared.tile([P, BLOCKS * H], U8, name="wp_sc_raw", offset=T, align_bytes=64)
-        nc.vector.memset(wp_sc_raw[:].bitcast(I32), 0)
         nc.vector.memset(tab_sc[:].bitcast(I32), 0)
+        nc.vector.memset(wp_sc_raw[:].bitcast(I32), 0)
         b1_sb = tile("b1_sb", [P, BLOCKS, 2 * PACK], F32)[:, :, :PACK]
         gd_sb = tile("gd_sb", [P, BLOCKS, 2 * PACK], F32)[:, :, :PACK]
         tab_w = [tile(f"tab_w{a}", [P, T], U32) for a in range(PASSES)]
@@ -75,7 +75,7 @@ def tile_list_cocoa_supply_tiers_kernel(
             )
 
         def load_wp_scales(q):
-            nc.sync.dma_start(
+            nc.gpsimd.dma_start(
                 out=wp_sc_raw[32 * q : 32 * q + 4, :].bitcast(I32).rearrange("r (a c) -> r a c", a=BLOCKS),
                 in_=wp_scales[:, 4 * q : 4 * q + 4, :].bitcast(I32).rearrange("a r c -> r a c"),
             )
@@ -138,7 +138,7 @@ def tile_list_cocoa_supply_tiers_kernel(
                 v_codes[a, half] = picked[:, i * BANK : (i + 1) * BANK]
 
         def cast_w(b, a, first, count, engines, tag):
-            w_bf[b, a, first] = tile(f"w_bf{b}{a}{first}", [P, PACK, P, PACK], BF16, tag=tag)[:, :count]
+            w_bf[b, a, first] = tile(f"w_bf{b}{a}{first}", [P, count, P, PACK], BF16, tag=tag)[:]
             share = count // len(engines)
             for i, engine in enumerate(engines):
                 t0 = i * share
@@ -154,9 +154,9 @@ def tile_list_cocoa_supply_tiers_kernel(
                     src = src.rearrange("p m j t -> p m t j")
                     nc.gpsimd.tensor_scalar(dst, src, 1.0, 0.0, ALU.mult, ALU.add)
 
-        def quantize_w(b, a, first):
+        def quantize_w(b, a, first, tag=None):
             count = w_bf[b, a, first].shape[1]
-            codes = tile(f"w_codes{b}{a}{first}", [P, count * P], U32)
+            codes = tile(f"w_codes{b}{a}{first}", [P, count * P], U32, tag=tag)
             scales = tile(f"w_scales{b}{a}{first}", [P, count * P], U8)
             nc.vector.quantize_mx(
                 out=codes[:].bitcast(FP8X4),
@@ -229,7 +229,6 @@ def tile_list_cocoa_supply_tiers_kernel(
             for i in range(count):
                 wp_codes[b, first + i] = dealt[:, :, i * 2 * P : (i + 1) * 2 * P]
 
-        wp_sc = tile("wp_sc", [P, BLOCKS * H], U8)
         y = {}
 
         def second_product(u, a):
@@ -262,6 +261,7 @@ def tile_list_cocoa_supply_tiers_kernel(
             cast_w(0, a, 0, PACK, ["scalar"], f"w_bf{a}")
             quantize_w(0, a, 0)
         first_product(0, 0, by_half)
+        wp_sc = tile("wp_sc", [P, BLOCKS * H], U8, tag="w_bf2")
         nc.vector.tensor_copy(
             wp_sc[:].rearrange("p (g t m) -> p g t m", t=PACK, m=P),
             wp_sc_raw[:].rearrange("p (g m t) -> p g t m", t=PACK, m=P),
@@ -277,21 +277,21 @@ def tile_list_cocoa_supply_tiers_kernel(
         cast_w(1, 0, 0, PACK, ["vector"], "w_bf0")
         quantize_w(1, 0, 0)
         first_product(1, 0, opening)
-        cast_w(1, 1, 0, 2, ["vector"], 16448)
+        cast_w(1, 1, 0, 2, ["vector"], 16256)
         quantize_w(1, 1, 0)
-        cast_w(1, 1, 2, 2, ["gpsimd"], 12416)
-        up_first = tile("up_first", [P, PACK, HALF_M], F32, tag=20480)
+        cast_w(1, 1, 2, 2, ["gpsimd"], 14272)
+        up_first = tile("up_first", [P, PACK, HALF_M], F32, tag=18240)
         for t in range(PACK):
             gather_up(up_first[:, t, :], 0, t, 0, HALF_M)
-        cast_w(1, 2, 0, 2, ["scalar"], 8320)
+        cast_w(1, 2, 0, 2, ["scalar"], 10240)
         quantize_w(1, 2, 0)
-        quantize_w(1, 1, 2)
-        cast_w(1, 2, 2, 2, ["gpsimd"], 12352)
+        quantize_w(1, 1, 2, tag=10304)
+        cast_w(1, 2, 2, 2, ["gpsimd"], 14272)
         quantize_w(1, 2, 2)
         for bank in by_slice:
             for a in (1, 2):
                 first_product(1, a, [bank])
-        x_first = round_x("x_first", up_first[:], 10304)
+        x_first = round_x("x_first", up_first[:], 12224)
         up_second = tile("up_second", [P, PACK, HALF_M], F32, tag=6208)
         for t in range(PACK):
             gather_up(up_second[:, t, :], 0, t, HALF_M, HALF_M)

@@ -56,8 +56,8 @@ def tile_list_cocoa_supply_tiers_kernel(
         wp_sc_raw = shared.tile([P, BLOCKS * H], U8, name="wp_sc_raw", offset=T, align_bytes=64)
         nc.vector.memset(tab_sc[:].bitcast(I32), 0)
         nc.vector.memset(wp_sc_raw[:].bitcast(I32), 0)
-        b1_sb = tile("b1_sb", [P, BLOCKS, 2 * PACK], F32)[:, :, :PACK]
-        gd_sb = tile("gd_sb", [P, BLOCKS, 2 * PACK], F32)[:, :, :PACK]
+        rows = tile("rows", [P, P], F32)
+        nc.vector.memset(rows[:], 0.0)
         tab_w = [tile(f"tab_w{a}", [P, T], U32) for a in range(PASSES)]
         w_raw = {(b, a): tile(f"w_raw{b}{a}", [P, PACK, KP], F32) for b in range(BLOCKS) for a in range(PASSES)}
         wp_raw = tile("wp_raw", [P, BLOCKS * 2 * H], U8)
@@ -87,16 +87,17 @@ def tile_list_cocoa_supply_tiers_kernel(
                 out=tab_sc[32 * q + 4 : 32 * q + 4 + 4 * PASSES, :].bitcast(I32),
                 in_=tab_scales[:, 4 * q : 4 * q + 4, :].bitcast(I32),
             )
-        nc.scalar.dma_start(out=gd_sb, in_=gd.rearrange("(b p t) -> p b t", p=P, t=PACK))
+        nc.scalar.dma_start(out=rows[1:P:16, :], in_=gd.rearrange("(b q c) -> q b c", b=BLOCKS, c=P))
         for a in range(PASSES):
             load_w(0, a)
-        nc.scalar.dma_start(out=b1_sb, in_=b1.rearrange("(b p t) -> p b t", p=P, t=PACK))
-        nc.sync.dma_start(pos1_sb[:], pos1)
+        nc.scalar.dma_start(out=rows[0:P:16, :], in_=b1.rearrange("(b q c) -> q b c", b=BLOCKS, c=P))
         for q in range(4):
             load_wp_scales(q)
         load_table(1)
         load_table(2)
-        for a in range(PASSES):
+        load_w(1, 0)
+        nc.sync.dma_start(pos1_sb[:], pos1)
+        for a in range(1, PASSES):
             load_w(1, a)
         nc.sync.dma_start(
             out=wp_raw[:].bitcast(I32).rearrange("p (a c) -> p a c", a=BLOCKS),
@@ -104,6 +105,14 @@ def tile_list_cocoa_supply_tiers_kernel(
         )
         nc.sync.dma_start(pos2_sb[:], pos2)
 
+        dealt_rows = tile("dealt_rows", [P, PACK, 32], F32)
+        columns = tile("columns", [P, PACK, BLOCKS, 16], F32)
+        nc.vector.tensor_copy(dealt_rows[:], rows[:].rearrange("p (j t) -> p t j", t=PACK))
+        nc.vector.transpose(
+            columns[:].rearrange("p t b i -> p (t b i)"), dealt_rows[:].rearrange("p t j -> p (t j)")
+        )
+        b1_sb = columns[:, :, :, 0].rearrange("p t b -> p b t")
+        gd_sb = columns[:, :, :, 1].rearrange("p t b -> p b t")
         gd_abs = tile("gd_abs", [P, BLOCKS, PACK], F32)
         gd_floor = tile("gd_floor", [P, BLOCKS, PACK], F32)
         gd_rsqrt = tile("gd_rsqrt", [P, BLOCKS, PACK], F32)
@@ -357,16 +366,16 @@ def tile_list_cocoa_supply_tiers_kernel(
 
         def finish(u, cols):
             b, ts, entries = UNITS[u]
-            rows = out[b * KP : (b + 1) * KP, :].rearrange("(p t) m -> p t m", t=PACK)
+            out_rows = out[b * KP : (b + 1) * KP, :].rearrange("(p t) m -> p t m", t=PACK)
             if u == n - 1:
                 nc.vector.tensor_tensor(res[:, u, cols], damp[:, u, cols], down[:, cols], ALU.mult)
-                nc.sync.dma_start(out=rows[:, ts[0], cols], in_=res[:, u, cols])
+                nc.sync.dma_start(out=out_rows[:, ts[0], cols], in_=res[:, u, cols])
                 return
             offsets = pos2_sb[:, entries.start // 16 : entries.stop // 16]
             for t, run in runs(u, cols):
                 nc.vector.tensor_tensor(res[:, u, run], h[b, t][:].indirect(offsets), damp[:, u, run], ALU.mult)
             nc.sync.dma_start(
-                out=rows[:, ts[0] : ts[-1] + 1, entries], in_=res[:, u, :].rearrange("p (t m) -> p t m", t=len(ts))
+                out=out_rows[:, ts[0] : ts[-1] + 1, entries], in_=res[:, u, :].rearrange("p (t m) -> p t m", t=len(ts))
             )
 
         magnitude(0, whole)

@@ -53,9 +53,11 @@ def tile_list_cocoa_supply_tiers_kernel(
         pos2_sb = lists.tile([P, M // 16], U16, name="pos2_sb")
 
         tab_sc = shared.tile([P, T], U8, name="tab_sc", offset=0, align_bytes=64)
-        wp_sc_raw = shared.tile([P, BLOCKS * H], U8, name="wp_sc_raw", offset=T, align_bytes=64)
+        wp_sc_raw = shared.tile([P, H], U8, name="wp_sc_raw", offset=T, align_bytes=64)
+        wp_sc = tile("wp_sc", [P, BLOCKS * H], U8)
         nc.vector.memset(tab_sc[:].bitcast(I32), 0)
         nc.vector.memset(wp_sc_raw[:].bitcast(I32), 0)
+        nc.vector.memset(wp_sc[:].bitcast(I32), 0)
         rows = tile("rows", [P, P], F32)
         nc.vector.memset(rows[:], 0.0)
         tab_w = [tile(f"tab_w{a}", [P, T], U32) for a in range(PASSES)]
@@ -74,12 +76,6 @@ def tile_list_cocoa_supply_tiers_kernel(
                 in_=w1[a * KP : (a + 1) * KP, b * KP : (b + 1) * KP].rearrange("(p j) c -> p j c", j=PACK),
             )
 
-        def load_wp_scales(q):
-            nc.gpsimd.dma_start(
-                out=wp_sc_raw[32 * q : 32 * q + 4, :].bitcast(I32).rearrange("r (a c) -> r a c", a=BLOCKS),
-                in_=wp_scales[:, 4 * q : 4 * q + 4, :].bitcast(I32).rearrange("a r c -> r a c"),
-            )
-
         nc.sync.dma_start(offs_sb[:], offs)
         load_table(0)
         for q in range(4):
@@ -91,8 +87,9 @@ def tile_list_cocoa_supply_tiers_kernel(
         for a in range(PASSES):
             load_w(0, a)
         nc.scalar.dma_start(out=rows[0:P:16, :], in_=b1.rearrange("(b q c) -> q b c", b=BLOCKS, c=P))
-        for q in range(4):
-            load_wp_scales(q)
+        nc.gpsimd.dma_start(
+            out=wp_sc_raw[0:P:4, :].bitcast(I32), in_=wp_scales.rearrange("a q c -> (a q) c").bitcast(I32)
+        )
         load_table(1)
         load_table(2)
         load_w(1, 0)
@@ -270,9 +267,9 @@ def tile_list_cocoa_supply_tiers_kernel(
             cast_w(0, a, 0, PACK, ["scalar"], f"w_bf{a}")
             quantize_w(0, a, 0)
         first_product(0, 0, by_half)
-        wp_sc = tile("wp_sc", [P, BLOCKS * H], U8, tag="w_bf2")
+        wp_sc_dealt = tile("wp_sc_dealt", [P, H], U8, tag="w_bf2")
         nc.vector.tensor_copy(
-            wp_sc[:].rearrange("p (g t m) -> p g t m", t=PACK, m=P),
+            wp_sc_dealt[:].rearrange("p (g t m) -> p g t m", t=PACK, m=P),
             wp_sc_raw[:].rearrange("p (g m t) -> p g t m", t=PACK, m=P),
         )
         for half in range(HALVES):
@@ -300,6 +297,13 @@ def tile_list_cocoa_supply_tiers_kernel(
         for bank in by_slice:
             for a in (1, 2):
                 first_product(1, a, [bank])
+        for a in range(BLOCKS):
+            for q in range(4):
+                first = 4 * (16 * a + 4 * q)
+                nc.sync.dma_start(
+                    out=wp_sc[32 * q : 32 * q + 4, a * H : (a + 1) * H].bitcast(I32),
+                    in_=wp_sc_dealt[first : first + 16 : 4, :].bitcast(I32),
+                )
         x_first = round_x("x_first", up_first[:], 12224)
         up_second = tile("up_second", [P, PACK, HALF_M], F32, tag=6208)
         for t in range(PACK):

@@ -27,9 +27,15 @@ HALF_M = M // 2
 SLICES = [(b, t) for b in range(BLOCKS) for t in range(PACK)]
 UNITS = [(0, (0, 1), slice(m0, m0 + HALF_M)) for m0 in (0, HALF_M)]
 UNITS = UNITS + [(b, (t,), slice(0, M)) for b, t in SLICES[2:]]
-LAST_RUNS = ((0, 128), (128, 128), (256, 256))
 SMALLEST_NORMAL = 2.0**-126
 SQUARED_ON_VECTOR = 3
+
+AT_TAB_SC = 0
+AT_WP_SC = 4096
+AT_SIGN = 22336
+AT_BIAS = 23360
+AT_UP_LAST = 23872
+AT_MAG = 32064
 
 
 def tile_list_cocoa_supply_tiers_kernel(
@@ -40,7 +46,6 @@ def tile_list_cocoa_supply_tiers_kernel(
         lists = ctx.enter_context(tc.tile_pool(name="lists", bufs=1))
         keep = ctx.enter_context(tc.tile_pool(name="keep", bufs=1))
         shared = ctx.enter_context(tc.tile_pool(name="shared", bufs=1))
-        ring = ctx.enter_context(tc.tile_pool(name="ring", bufs=3))
         psum = ctx.enter_context(tc.psum_pool(name="psum", bufs=1))
 
         def tile(name, shape, dtype, tag=None):
@@ -52,8 +57,8 @@ def tile_list_cocoa_supply_tiers_kernel(
         pos1_sb = lists.tile([P, M // 16], U16, name="pos1_sb")
         pos2_sb = lists.tile([P, M // 16], U16, name="pos2_sb")
 
-        tab_sc = shared.tile([P, T], U8, name="tab_sc", offset=0, align_bytes=64)
-        wp_sc_raw = shared.tile([P, H], U8, name="wp_sc_raw", offset=T, align_bytes=64)
+        tab_sc = tile("tab_sc", [P, T], U8, tag=AT_TAB_SC)
+        wp_sc_raw = tile("wp_sc_raw", [P, H], U8, tag=AT_WP_SC)
         wp_sc = tile("wp_sc", [P, BLOCKS * H], U8)
         nc.vector.memset(tab_sc[:].bitcast(I32), 0)
         nc.vector.memset(wp_sc_raw[:].bitcast(I32), 0)
@@ -61,7 +66,11 @@ def tile_list_cocoa_supply_tiers_kernel(
         rows = tile("rows", [P, P], F32)
         nc.vector.memset(rows[:], 0.0)
         tab_w = [tile(f"tab_w{a}", [P, T], U32) for a in range(PASSES)]
-        w_raw = {(b, a): tile(f"w_raw{b}{a}", [P, PACK, KP], F32) for b in range(BLOCKS) for a in range(PASSES)}
+        w_raw = {
+            (b, a): tile(f"w_raw{b}{a}", [P, PACK, KP], F32)
+            for b in range(BLOCKS)
+            for a in range(PASSES)
+        }
         wp_raw = tile("wp_raw", [P, BLOCKS * 2 * H], U8)
 
         def load_table(a):
@@ -94,8 +103,8 @@ def tile_list_cocoa_supply_tiers_kernel(
         load_table(2)
         load_w(1, 0)
         nc.sync.dma_start(pos1_sb[:], pos1)
-        for a in range(1, PASSES):
-            load_w(1, a)
+        load_w(1, 1)
+        load_w(1, 2)
         nc.sync.dma_start(
             out=wp_raw[:].bitcast(I32).rearrange("p (a c) -> p a c", a=BLOCKS),
             in_=wp_words.bitcast(I32).rearrange("a p c -> p a c"),
@@ -115,8 +124,8 @@ def tile_list_cocoa_supply_tiers_kernel(
         gd_rsqrt = tile("gd_rsqrt", [P, BLOCKS, PACK], F32)
         gd_root = tile("gd_root", [P, BLOCKS, PACK], F32)
         positive = tile("positive", [P, BLOCKS, PACK], F32)
-        sign = tile("sign", [P, BLOCKS, PACK], F32)
-        b1_signed = tile("b1_signed", [P, BLOCKS, PACK], F32)
+        sign = tile("sign", [P, BLOCKS, PACK], F32, tag=AT_SIGN)
+        b1_signed = tile("b1_signed", [P, BLOCKS, PACK], F32, tag=AT_BIAS)
         nc.vector.tensor_scalar(positive[:], gd_sb, 0.0, None, ALU.is_ge)
         nc.vector.tensor_scalar(sign[:], positive[:], 2.0, -1.0, ALU.mult, ALU.add)
         nc.vector.tensor_tensor(gd_abs[:], gd_sb, sign[:], ALU.mult)
@@ -129,49 +138,39 @@ def tile_list_cocoa_supply_tiers_kernel(
         v_scales = tile("v_scales", [P, S], U8)
         w_codes = {}
         w_scales = {}
-        w_bf = {}
 
         def gather_table(a, halves):
             first, count = halves[0], len(halves)
-            if a == 1:
-                picked = shared.tile([P, BANK], U32, name=f"v_codes1{first}", offset=first * T, align_bytes=64)
-            else:
-                picked = tile(f"v_codes{a}{first}", [P, count * BANK], U32)
+            place = (AT_TAB_SC, AT_WP_SC)[first] if a == 1 else None
+            picked = tile(f"v_codes{a}{first}", [P, count * BANK], U32, tag=place)
             nc.vector.tensor_copy(
                 picked[:], tab_w[a][:].indirect(offs_sb[:, first * BANK // 16 : (first + count) * BANK // 16])
             )
             for i, half in enumerate(halves):
                 v_codes[a, half] = picked[:, i * BANK : (i + 1) * BANK]
 
-        def cast_w(b, a, first, count, engines, tag):
-            w_bf[b, a, first] = tile(f"w_bf{b}{a}{first}", [P, count, P, PACK], BF16, tag=tag)[:]
-            share = count // len(engines)
-            for i, engine in enumerate(engines):
-                t0 = i * share
-                dst = w_bf[b, a, first][:, t0 : t0 + share].rearrange("p t m j -> p m j t")
-                src = w_raw[b, a][:].rearrange("p j (m t) -> p m j t", t=PACK)
-                src = src[:, :, :, first + t0 : first + t0 + share]
-                if engine == "scalar":
-                    nc.scalar.activation(dst, src, ACT.Copy)
-                elif engine == "vector":
-                    nc.vector.tensor_copy(dst, src)
-                else:
-                    dst = dst.rearrange("p m j t -> p m t j")
-                    src = src.rearrange("p m j t -> p m t j")
-                    nc.gpsimd.tensor_scalar(dst, src, 1.0, 0.0, ALU.mult, ALU.add)
+        def cast_w(engine, w_bf, b, a, first):
+            count = w_bf.shape[1]
+            dst = w_bf.rearrange("p t m j -> p m j t")
+            src = w_raw[b, a][:].rearrange("p j (m t) -> p m j t", t=PACK)[:, :, :, first : first + count]
+            if engine == "scalar":
+                nc.scalar.activation(dst, src, ACT.Copy)
+            elif engine == "vector":
+                nc.vector.tensor_copy(dst, src)
+            else:
+                dst = dst.rearrange("p m j t -> p m t j")
+                src = src.rearrange("p m j t -> p m t j")
+                nc.gpsimd.tensor_scalar(dst, src, 1.0, 0.0, ALU.mult, ALU.add)
 
-        def quantize_w(b, a, first, tag=None):
-            count = w_bf[b, a, first].shape[1]
-            codes = tile(f"w_codes{b}{a}{first}", [P, count * P], U32, tag=tag)
-            scales = tile(f"w_scales{b}{a}{first}", [P, count * P], U8)
+        def quantize_w(name, w_bf, keys, tag=None):
+            codes = tile(f"w_codes{name}", [P, len(keys) * P], U32, tag=tag)
+            scales = tile(f"w_scales{name}", [P, len(keys) * P], U8)
             nc.vector.quantize_mx(
-                out=codes[:].bitcast(FP8X4),
-                scales=scales[:],
-                in_=w_bf[b, a, first].rearrange("p t m j -> p (t m j)"),
+                out=codes[:].bitcast(FP8X4), scales=scales[:], in_=w_bf[:].rearrange("p t m j -> p (t m j)")
             )
-            for i in range(count):
-                w_codes[b, a, first + i] = codes[:, i * P : (i + 1) * P]
-                w_scales[b, a, first + i] = scales[:, i * P : (i + 1) * P]
+            for i, key in enumerate(keys):
+                w_codes[key] = codes[:, i * P : (i + 1) * P]
+                w_scales[key] = scales[:, i * P : (i + 1) * P]
 
         banks = {}
 
@@ -200,28 +199,24 @@ def tile_list_cocoa_supply_tiers_kernel(
                 scale=sign[:, b, t : t + 1],
             )
 
-        x_codes = {1: tile("x_codes1", [P, M], U32)}
-        x_scales = [tile(f"x_scales{b}", [P, M], U8) for b in range(BLOCKS)]
+        x_codes = [tile(f"x_codes{b}", [P, M], U32) for b in range(BLOCKS)]
+        x_scales = {1: tile("x_scales1", [P, M], U8)}
 
         def gather_up(dst, b, t, m0, width):
             nc.vector.tensor_copy(dst, h[b, t][:].indirect(pos1_sb[:, m0 // 16 : (m0 + width) // 16]))
 
-        def round_x(name, up, tag, pieces=1):
-            x_bf = tile(name, [P, HALF_M, PACK], BF16, tag=tag)
-            for i in range(pieces):
-                cols = slice(i * HALF_M // pieces, (i + 1) * HALF_M // pieces)
-                nc.scalar.activation(
-                    x_bf[:, cols].rearrange("p (c i) t -> p c t i", i=4),
-                    up[:, :, cols].rearrange("p t (c i) -> p c t i", i=4),
-                    ACT.Abs,
-                )
-            return x_bf
+        def round_x(x_bf, up):
+            nc.scalar.activation(
+                x_bf.rearrange("p (c i) t -> p c t i", i=4),
+                up.rearrange("p t (c i) -> p c t i", i=4),
+                ACT.Abs,
+            )
 
         def quantize_x(b, m0, x_bf):
             nc.vector.quantize_mx(
                 out=x_codes[b][:, m0 : m0 + HALF_M].bitcast(FP8X4),
                 scales=x_scales[b][:, m0 : m0 + HALF_M],
-                in_=x_bf[:].rearrange("p m t -> p (m t)"),
+                in_=x_bf.rearrange("p m t -> p (m t)"),
             )
 
         wp_codes = {}
@@ -237,15 +232,14 @@ def tile_list_cocoa_supply_tiers_kernel(
 
         y = {}
 
-        def second_product(u, a):
+        def second_product(u, a, first):
             b, ts, entries = UNITS[u]
-            if a == 0:
+            if first:
                 y[u] = psum.tile([P, BANK], F32, name=f"bank{u}")
-            width = BANK if len(ts) == 1 else P
-            count = BANK // width
-            for i in range(count):
-                t = ts[i * len(ts) // count]
-                m0 = entries.start + i % 2 * width
+            count = len(ts)
+            width = BANK // count
+            m0 = entries.start
+            for i, t in enumerate(ts):
                 c0 = a * H + b * KP + t * P
                 nc.tensor.matmul_mx(
                     out=y[u][:, i * width : (i + 1) * width],
@@ -253,19 +247,20 @@ def tile_list_cocoa_supply_tiers_kernel(
                     lhsT_scale=wp_sc[:, c0 : c0 + P],
                     rhs=x_codes[a][:, m0 : m0 + width].bitcast(FP8X4),
                     rhs_scale=x_scales[a][:, m0 : m0 + width],
-                    start=(a, i) == (0, 0),
-                    stop=(a, i) == (BLOCKS - 1, count - 1),
+                    start=first and i == 0,
+                    stop=not first and i == count - 1,
                 )
 
         by_half = [(t, half) for half in range(HALVES) for t in range(PACK)]
         by_slice = [(t, half) for t in range(PACK) for half in range(HALVES)]
-
         opening = [(0, 0), (1, 0), (0, 1), (1, 1)] + by_slice[4:]
+
         gather_table(0, (0, 1))
         nc.vector.tensor_copy(v_scales[:], tab_sc[:].indirect(offs_sb[:]))
         for a in range(PASSES):
-            cast_w(0, a, 0, PACK, ["scalar"], f"w_bf{a}")
-            quantize_w(0, a, 0)
+            w_bf = tile(f"w_bf0{a}", [P, PACK, P, PACK], BF16, tag=f"w_bf{a}")
+            cast_w("scalar", w_bf[:], 0, a, 0)
+            quantize_w(f"0{a}", w_bf, [(0, a, t) for t in range(PACK)])
         first_product(0, 0, by_half)
         wp_sc_dealt = tile("wp_sc_dealt", [P, H], U8, tag="w_bf2")
         nc.vector.tensor_copy(
@@ -280,20 +275,31 @@ def tile_list_cocoa_supply_tiers_kernel(
         first_product(0, 2, opening)
         for t, half in opening:
             empty_h(0, t, half)
-        cast_w(1, 0, 0, PACK, ["vector"], "w_bf0")
-        quantize_w(1, 0, 0)
+
+        w_bf10 = tile("w_bf10", [P, PACK, P, PACK], BF16, tag="w_bf0")
+        cast_w("vector", w_bf10[:], 1, 0, 0)
+        quantize_w("10", w_bf10, [(1, 0, t) for t in range(PACK)])
         first_product(1, 0, opening)
-        cast_w(1, 1, 0, 2, ["vector"], 16256)
-        quantize_w(1, 1, 0)
-        cast_w(1, 1, 2, 2, ["gpsimd"], 14272)
+        w_bf11 = tile("w_bf11", [P, 2, P, PACK], BF16, tag=16256)
+        cast_w("vector", w_bf11[:], 1, 1, 0)
+        quantize_w("11", w_bf11, [(1, 1, 0), (1, 1, 1)])
+        w_bf11b = tile("w_bf11b", [P, 2, P, PACK], BF16, tag=14272)
+        cast_w("gpsimd", w_bf11b[:], 1, 1, 2)
         up_first = tile("up_first", [P, PACK, HALF_M], F32, tag=18240)
         for t in range(PACK):
             gather_up(up_first[:, t, :], 0, t, 0, HALF_M)
-        cast_w(1, 2, 0, 2, ["scalar"], 10240)
-        quantize_w(1, 2, 0)
-        quantize_w(1, 1, 2, tag=10304)
-        cast_w(1, 2, 2, 2, ["gpsimd"], 14272)
-        quantize_w(1, 2, 2)
+        w_bf12 = tile("w_bf12", [P, 2, P, PACK], BF16, tag=10240)
+        cast_w("scalar", w_bf12[:], 1, 2, 0)
+        quantize_w("12", w_bf12, [(1, 2, 0), (1, 2, 1)])
+        quantize_w("11b", w_bf11b, [(1, 1, 2), (1, 1, 3)], 10304)
+        w_bf12b = tile("w_bf12b", [P, 2, P, PACK], BF16, tag=14272)
+        cast_w("gpsimd", w_bf12b[:], 1, 2, 2)
+        x_first = tile("x_first", [P, HALF_M, PACK], BF16, tag=12224)
+        round_x(x_first[:], up_first[:])
+        up_second = tile("up_second", [P, PACK, HALF_M], F32, tag=6208)
+        for t in range(PACK):
+            gather_up(up_second[:, t, :], 0, t, HALF_M, HALF_M)
+        quantize_w("12b", w_bf12b, [(1, 2, 2), (1, 2, 3)])
         for bank in by_slice:
             for a in (1, 2):
                 first_product(1, a, [bank])
@@ -304,38 +310,34 @@ def tile_list_cocoa_supply_tiers_kernel(
                     out=wp_sc[32 * q : 32 * q + 4, a * H : (a + 1) * H].bitcast(I32),
                     in_=wp_sc_dealt[first : first + 16 : 4, :].bitcast(I32),
                 )
-        x_first = round_x("x_first", up_first[:], 12224)
-        up_second = tile("up_second", [P, PACK, HALF_M], F32, tag=6208)
-        for t in range(PACK):
-            gather_up(up_second[:, t, :], 0, t, HALF_M, HALF_M)
-        up_last = tile("up_last", [P, PACK, M], F32)
+        up_last = tile("up_last", [P, PACK, M], F32, tag=AT_UP_LAST)
         for t in range(PACK):
             for half in range(HALVES):
                 empty_h(1, t, half)
-            if t < PACK - 1:
-                gather_up(up_last[:, t, :], 1, t, 0, M)
-            else:
-                for m0, width in LAST_RUNS:
-                    gather_up(up_last[:, t, m0 : m0 + width], 1, t, m0, width)
-        x_second = round_x("x_second", up_second[:], "w_codes122")
-        x_codes[0] = tile("x_codes0", [P, M], U32, tag=7232)
-        quantize_x(0, 0, x_first)
-        deal_wp_words(0, 0, 2, 6208)
-        second_product(0, 0)
-        x_third = round_x("x_third", up_last[:, :, :HALF_M], "x_third", pieces=2)
-        quantize_x(1, 0, x_third)
-        second_product(0, 1)
-        quantize_x(0, HALF_M, x_second)
-        second_product(1, 0)
-        x_fourth = round_x("x_fourth", up_last[:, :, HALF_M:], 2048)
-        quantize_x(1, HALF_M, x_fourth)
-        second_product(1, 1)
-        deal_wp_words(0, 2, 2, 2112)
-        deal_wp_words(1, 0, PACK, 64)
+            gather_up(up_last[:, t, : M if t < PACK - 1 else HALF_M], 1, t, 0, M if t < PACK - 1 else HALF_M)
+        deal_wp_words(0, 0, 2, AT_SIGN)
+        x_scales[0] = tile("x_scales0", [P, M], U8, tag=AT_BIAS)
+        quantize_x(0, 0, x_first[:])
+        second_product(0, 0, True)
+        gather_up(up_last[:, PACK - 1, HALF_M:], 1, PACK - 1, HALF_M, HALF_M)
+        x_second = tile("x_second", [P, HALF_M, PACK], BF16, tag="w_codes12b")
+        round_x(x_second[:], up_second[:])
+        quantize_x(0, HALF_M, x_second[:])
+        second_product(1, 0, True)
+        x_third = tile("x_third", [P, HALF_M, PACK], BF16)
+        round_x(x_third[:], up_last[:, :, :HALF_M])
+        quantize_x(1, 0, x_third[:])
+        second_product(0, 1, False)
+        deal_wp_words(0, 2, 2, "x_third")
+        x_fourth = tile("x_fourth", [P, HALF_M, PACK], BF16)
+        round_x(x_fourth[:], up_last[:, :, HALF_M:])
+        quantize_x(1, HALF_M, x_fourth[:])
+        second_product(1, 1, False)
+        deal_wp_words(1, 0, PACK, AT_UP_LAST)
         for u in range(2, len(UNITS)):
-            for a in range(BLOCKS):
-                second_product(u, a)
-        down = tile("down", [P, M], F32, tag=3136)
+            second_product(u, 1, True)
+            second_product(u, 0, False)
+        down = tile("down", [P, M], F32, tag=AT_UP_LAST + 2048)
         nc.vector.tensor_copy(down[:], h[SLICES[-1]][:].indirect(pos2_sb[:]))
 
         n = len(UNITS)
@@ -344,21 +346,21 @@ def tile_list_cocoa_supply_tiers_kernel(
         mag = {}
         roots = tile("roots", [P, n, M], F32, tag="tab_w0")
         damp = tile("damp", [P, n, M], F32, tag="tab_w1")
-        res = tile("res", [P, n, M], F32, tag="tab_w2")
+        results = tile("results", [P, n, M], F32, tag="tab_w2")
 
         def runs(u, cols):
             ts = UNITS[u][1]
             return [(ts[0], cols)] if len(ts) == 1 else list(zip(ts, halves))
 
-        def magnitude(u, cols):
+        def magnitude(u, cols=whole):
             if u not in mag:
-                mag[u] = ring.tile([P, M], F32, name="mag")
+                mag[u] = tile(f"mag{u}", [P, M], F32, tag=AT_MAG + 2048 if u == 2 else None)
             nc.scalar.activation(mag[u][:, cols], y[u][:, cols], ACT.Abs)
 
-        def root(u, cols):
+        def root(u, cols=whole):
             nc.scalar.activation(roots[:, u, cols], mag[u][:, cols], ACT.Abs_reciprocal_sqrt, bias=1.0)
 
-        def square(u, cols):
+        def square(u, cols=whole):
             b = UNITS[u][0]
             for t, run in runs(u, cols):
                 if u < SQUARED_ON_VECTOR:
@@ -368,26 +370,46 @@ def tile_list_cocoa_supply_tiers_kernel(
                 else:
                     nc.scalar.activation(damp[:, u, run], roots[:, u, run], ACT.Square, scale=gd_root[:, b, t : t + 1])
 
-        def finish(u, cols):
+        def finish(u, cols=whole):
             b, ts, entries = UNITS[u]
             out_rows = out[b * KP : (b + 1) * KP, :].rearrange("(p t) m -> p t m", t=PACK)
+            if 1 <= u < SQUARED_ON_VECTOR - 1:
+                res = tile(f"res{u}", [P, M], F32, tag=AT_MAG + 2048 if u == 1 else f"mag{u + 1}")[:]
+            else:
+                res = results[:, u, :]
             if u == n - 1:
-                nc.vector.tensor_tensor(res[:, u, cols], damp[:, u, cols], down[:, cols], ALU.mult)
-                nc.sync.dma_start(out=out_rows[:, ts[0], cols], in_=res[:, u, cols])
+                nc.vector.tensor_tensor(res[:, cols], damp[:, u, cols], down[:, cols], ALU.mult)
+                nc.sync.dma_start(out=out_rows[:, ts[0], cols], in_=res[:, cols])
                 return
             offsets = pos2_sb[:, entries.start // 16 : entries.stop // 16]
             for t, run in runs(u, cols):
-                nc.vector.tensor_tensor(res[:, u, run], h[b, t][:].indirect(offsets), damp[:, u, run], ALU.mult)
+                nc.vector.tensor_tensor(res[:, run], h[b, t][:].indirect(offsets), damp[:, u, run], ALU.mult)
             nc.sync.dma_start(
-                out=out_rows[:, ts[0] : ts[-1] + 1, entries], in_=res[:, u, :].rearrange("p (t m) -> p t m", t=len(ts))
+                out=out_rows[:, ts[0] : ts[-1] + 1, entries], in_=res.rearrange("p (t m) -> p t m", t=len(ts))
             )
 
-        magnitude(0, whole)
-        for u in range(n - 1):
-            root(u, whole)
+        magnitude(0)
+        root(0)
+        square(0)
+        finish(0)
+        for u in (1, 3):
+            magnitude(u)
+            magnitude(u + 1)
+            root(u)
+            root(u + 1)
+            if u == 1:
+                square(1)
+                square(2)
+                finish(1)
+        finish(2)
+        square(3)
+        finish(3)
+        for u in range(4, n - 1):
             magnitude(u + 1, whole if u + 1 < n - 1 else halves[0])
-            square(u, whole)
-            finish(u, whole)
+            square(u)
+            finish(u)
+            if u + 1 < n - 1:
+                root(u + 1)
         magnitude(n - 1, halves[1])
         for cols in halves:
             root(n - 1, cols)

@@ -207,8 +207,8 @@ def tile_list_cocoa_supply_tiers_kernel(
 
         def round_x(x_bf, up):
             nc.scalar.activation(
-                x_bf.rearrange("p (c i) t -> p c t i", i=4),
-                up.rearrange("p t (c i) -> p c t i", i=4),
+                x_bf.rearrange("p (c i) t -> p c t i", i=2),
+                up.rearrange("p t (c i) -> p c t i", i=2),
                 ACT.Abs,
             )
 

@@ -26,9 +26,10 @@ HALVES = S // BANK
 HALF_M = M // 2
 SLICES = [(b, t) for b in range(BLOCKS) for t in range(PACK)]
 UNITS = [(0, (0, 1), slice(m0, m0 + HALF_M)) for m0 in (0, HALF_M)]
-UNITS = UNITS + [(b, (t,), slice(0, M)) for b, t in SLICES[2:]]
+UNITS = UNITS + [(b, (t,), slice(0, M)) for b, t in SLICES[4:7] + SLICES[2:4] + SLICES[7:]]
 SMALLEST_NORMAL = 2.0**-126
 SQUARED_ON_VECTOR = 3
+GPSIMD_COLS = 64
 
 AT_TAB_SC = 0
 AT_WP_SC = 4096
@@ -102,8 +103,8 @@ def tile_list_cocoa_supply_tiers_kernel(
         load_table(1)
         load_table(2)
         load_w(1, 0)
-        nc.sync.dma_start(pos1_sb[:], pos1)
         load_w(1, 1)
+        nc.sync.dma_start(pos1_sb[:], pos1)
         load_w(1, 2)
         nc.sync.dma_start(
             out=wp_raw[:].bitcast(I32).rearrange("p (a c) -> p a c", a=BLOCKS),
@@ -149,10 +150,10 @@ def tile_list_cocoa_supply_tiers_kernel(
             for i, half in enumerate(halves):
                 v_codes[a, half] = picked[:, i * BANK : (i + 1) * BANK]
 
-        def cast_w(engine, w_bf, b, a, first):
+        def cast_w(engine, w_bf, b, a, first, cols=slice(0, P)):
             count = w_bf.shape[1]
-            dst = w_bf.rearrange("p t m j -> p m j t")
-            src = w_raw[b, a][:].rearrange("p j (m t) -> p m j t", t=PACK)[:, :, :, first : first + count]
+            dst = w_bf.rearrange("p t m j -> p m j t")[:, cols]
+            src = w_raw[b, a][:].rearrange("p j (m t) -> p m j t", t=PACK)[:, cols, :, first : first + count]
             if engine == "scalar":
                 nc.scalar.activation(dst, src, ACT.Copy)
             elif engine == "vector":
@@ -280,12 +281,14 @@ def tile_list_cocoa_supply_tiers_kernel(
         cast_w("vector", w_bf10[:], 1, 0, 0)
         quantize_w("10", w_bf10, [(1, 0, t) for t in range(PACK)])
         first_product(1, 0, opening)
-        w_bf11 = tile("w_bf11", [P, 2, P, PACK], BF16, tag=16256)
-        cast_w("vector", w_bf11[:], 1, 1, 0)
+        pairs = tile("pairs", [P, (4 * P - GPSIMD_COLS) * PACK], BF16, tag=14272)
+        w_bf11 = pairs[:, : 2 * P * PACK].rearrange("p (t m j) -> p t m j", t=2, j=PACK)
+        w_bf11b = pairs[:, (2 * P - GPSIMD_COLS) * PACK :].rearrange("p (t m j) -> p t m j", t=2, j=PACK)
+        cast_w("vector", w_bf11, 1, 1, 0)
+        cast_w("vector", w_bf11b, 1, 1, 2, slice(GPSIMD_COLS, P))
         quantize_w("11", w_bf11, [(1, 1, 0), (1, 1, 1)])
-        w_bf11b = tile("w_bf11b", [P, 2, P, PACK], BF16, tag=14272)
-        cast_w("gpsimd", w_bf11b[:], 1, 1, 2)
-        up_first = tile("up_first", [P, PACK, HALF_M], F32, tag=18240)
+        cast_w("gpsimd", w_bf11b, 1, 1, 2, slice(0, GPSIMD_COLS))
+        up_first = tile("up_first", [P, PACK, HALF_M], F32)
         for t in range(PACK):
             gather_up(up_first[:, t, :], 0, t, 0, HALF_M)
         w_bf12 = tile("w_bf12", [P, 2, P, PACK], BF16, tag=10240)
@@ -328,12 +331,12 @@ def tile_list_cocoa_supply_tiers_kernel(
         round_x(x_third[:], up_last[:, :, :HALF_M])
         quantize_x(1, 0, x_third[:])
         second_product(0, 1, False)
-        deal_wp_words(0, 2, 2, "x_third")
+        deal_wp_words(1, 0, PACK, "x_third")
         x_fourth = tile("x_fourth", [P, HALF_M, PACK], BF16)
         round_x(x_fourth[:], up_last[:, :, HALF_M:])
         quantize_x(1, HALF_M, x_fourth[:])
         second_product(1, 1, False)
-        deal_wp_words(1, 0, PACK, AT_UP_LAST)
+        deal_wp_words(0, 2, 2, AT_UP_LAST)
         for u in range(2, len(UNITS)):
             second_product(u, 1, True)
             second_product(u, 0, False)

@@ -29,14 +29,21 @@ UNITS = [(0, (0, 1), slice(m0, m0 + HALF_M)) for m0 in (0, HALF_M)]
 UNITS = UNITS + [(b, (t,), slice(0, M)) for b, t in SLICES[4:7] + SLICES[2:4] + SLICES[7:]]
 SMALLEST_NORMAL = 2.0**-126
 SQUARED_ON_VECTOR = 3
-GPSIMD_COLS = 64
+GPSIMD_COLS = 60
+FIRST_COLS = 80
+SECOND_COLS = 48
+SCALAR_COLS = 72
+GPSIMD_LAST_COLS = 64
+RAW = PACK * KP
 
 AT_TAB_SC = 0
 AT_WP_SC = 4096
-AT_SIGN = 22336
-AT_BIAS = 23360
-AT_UP_LAST = 23872
-AT_MAG = 32064
+AT_WP_WORDS = 6144
+AT_DEALT_SC = 12224
+AT_SIGN = 13248
+AT_BIAS = 14272
+AT_UP_LAST = 14784
+AT_MAG = 22976
 
 
 def tile_list_cocoa_supply_tiers_kernel(
@@ -59,20 +66,27 @@ def tile_list_cocoa_supply_tiers_kernel(
         pos2_sb = lists.tile([P, M // 16], U16, name="pos2_sb")
 
         tab_sc = tile("tab_sc", [P, T], U8, tag=AT_TAB_SC)
-        wp_sc_raw = tile("wp_sc_raw", [P, H], U8, tag=AT_WP_SC)
+        wp_sc_raw = [tile(f"wp_sc_raw{a}", [P, H], U8, tag=(AT_WP_SC, AT_WP_WORDS)[a]) for a in range(BLOCKS)]
         wp_sc = tile("wp_sc", [P, BLOCKS * H], U8)
         nc.vector.memset(tab_sc[:].bitcast(I32), 0)
-        nc.vector.memset(wp_sc_raw[:].bitcast(I32), 0)
+        for a in range(BLOCKS):
+            nc.vector.memset(wp_sc_raw[a][:].bitcast(I32), 0)
         nc.vector.memset(wp_sc[:].bitcast(I32), 0)
         rows = tile("rows", [P, P], F32)
         nc.vector.memset(rows[:], 0.0)
         tab_w = [tile(f"tab_w{a}", [P, T], U32) for a in range(PASSES)]
+        stage = tile("stage", [P, RAW + (PACK - 1) * HALF_M], F32)
         w_raw = {
-            (b, a): tile(f"w_raw{b}{a}", [P, PACK, KP], F32)
+            (b, a): tile(f"w_raw{b}{a}", [P, RAW], F32)[:]
             for b in range(BLOCKS)
             for a in range(PASSES)
+            if (b, a) != (1, 0)
         }
-        wp_raw = tile("wp_raw", [P, BLOCKS * 2 * H], U8)
+        w_raw[1, 0] = stage[:, :RAW]
+        up_first = stage[:, : PACK * HALF_M].rearrange("p (t m) -> p t m", t=PACK)
+        up_second = stage[:, RAW - HALF_M :].rearrange("p (t m) -> p t m", t=PACK)
+        w_bf12 = stage[:, RAW + P : RAW + P + KP].bitcast(BF16).rearrange("p (t m j) -> p t m j", t=2, j=PACK)
+        wp_raw = tile("wp_raw", [P, BLOCKS * 2 * H], U8, tag=AT_WP_WORDS)
 
         def load_table(a):
             nc.sync.dma_start(
@@ -82,7 +96,7 @@ def tile_list_cocoa_supply_tiers_kernel(
 
         def load_w(b, a):
             nc.sync.dma_start(
-                out=w_raw[b, a][:],
+                out=w_raw[b, a].rearrange("p (j c) -> p j c", j=PACK),
                 in_=w1[a * KP : (a + 1) * KP, b * KP : (b + 1) * KP].rearrange("(p j) c -> p j c", j=PACK),
             )
 
@@ -94,23 +108,18 @@ def tile_list_cocoa_supply_tiers_kernel(
                 in_=tab_scales[:, 4 * q : 4 * q + 4, :].bitcast(I32),
             )
         nc.scalar.dma_start(out=rows[1:P:16, :], in_=gd.rearrange("(b q c) -> q b c", b=BLOCKS, c=P))
-        for a in range(PASSES):
-            load_w(0, a)
+        load_w(0, 1)
+        load_w(0, 2)
         nc.scalar.dma_start(out=rows[0:P:16, :], in_=b1.rearrange("(b q c) -> q b c", b=BLOCKS, c=P))
-        nc.gpsimd.dma_start(
-            out=wp_sc_raw[0:P:4, :].bitcast(I32), in_=wp_scales.rearrange("a q c -> (a q) c").bitcast(I32)
-        )
+        for a in range(BLOCKS):
+            nc.gpsimd.dma_start(out=wp_sc_raw[a][4 * a : P : 8, :].bitcast(I32), in_=wp_scales[a].bitcast(I32))
         load_table(1)
         load_table(2)
+        load_w(0, 0)
         load_w(1, 0)
-        load_w(1, 1)
         nc.sync.dma_start(pos1_sb[:], pos1)
+        load_w(1, 1)
         load_w(1, 2)
-        nc.sync.dma_start(
-            out=wp_raw[:].bitcast(I32).rearrange("p (a c) -> p a c", a=BLOCKS),
-            in_=wp_words.bitcast(I32).rearrange("a p c -> p a c"),
-        )
-        nc.sync.dma_start(pos2_sb[:], pos2)
 
         dealt_rows = tile("dealt_rows", [P, PACK, 32], F32)
         columns = tile("columns", [P, PACK, BLOCKS, 16], F32)
@@ -153,7 +162,7 @@ def tile_list_cocoa_supply_tiers_kernel(
         def cast_w(engine, w_bf, b, a, first, cols=slice(0, P)):
             count = w_bf.shape[1]
             dst = w_bf.rearrange("p t m j -> p m j t")[:, cols]
-            src = w_raw[b, a][:].rearrange("p j (m t) -> p m j t", t=PACK)[:, cols, :, first : first + count]
+            src = w_raw[b, a].rearrange("p (j m t) -> p m j t", j=PACK, t=PACK)[:, cols, :, first : first + count]
             if engine == "scalar":
                 nc.scalar.activation(dst, src, ACT.Copy)
             elif engine == "vector":
@@ -163,11 +172,11 @@ def tile_list_cocoa_supply_tiers_kernel(
                 src = src.rearrange("p m j t -> p m t j")
                 nc.gpsimd.tensor_scalar(dst, src, 1.0, 0.0, ALU.mult, ALU.add)
 
-        def quantize_w(name, w_bf, keys, tag=None):
+        def quantize_w(name, w_bf, keys, tag=None, scale_tag=None):
             codes = tile(f"w_codes{name}", [P, len(keys) * P], U32, tag=tag)
-            scales = tile(f"w_scales{name}", [P, len(keys) * P], U8)
+            scales = tile(f"w_scales{name}", [P, len(keys) * P], U8, tag=scale_tag)
             nc.vector.quantize_mx(
-                out=codes[:].bitcast(FP8X4), scales=scales[:], in_=w_bf[:].rearrange("p t m j -> p (t m j)")
+                out=codes[:].bitcast(FP8X4), scales=scales[:], in_=w_bf.rearrange("p t m j -> p (t m j)")
             )
             for i, key in enumerate(keys):
                 w_codes[key] = codes[:, i * P : (i + 1) * P]
@@ -177,7 +186,8 @@ def tile_list_cocoa_supply_tiers_kernel(
 
         def first_product(b, a, order):
             for t, half in order:
-                if a == 0:
+                passes = (0, 1, 2) if b == 1 else ((1, 2, 0), (1, 0, 2))[half]
+                if a == passes[0]:
                     banks[b, t, half] = psum.tile([P, BANK], F32, name=f"bank{HALVES * t + half}")
                 nc.tensor.matmul_mx(
                     out=banks[b, t, half][:],
@@ -185,20 +195,19 @@ def tile_list_cocoa_supply_tiers_kernel(
                     lhsT_scale=w_scales[b, a, t],
                     rhs=v_codes[a, half].bitcast(FP8X4),
                     rhs_scale=v_scales[4 * (a + 1) : P, half * BANK : (half + 1) * BANK],
-                    start=(a == 0),
-                    stop=(a == PASSES - 1),
+                    start=(a == passes[0]),
+                    stop=(a == passes[-1]),
                 )
 
         h = {(b, t): tile(f"h{b}{t}", [P, S], F32) for b, t in SLICES}
 
-        def empty_h(b, t, half):
-            nc.scalar.activation(
-                h[b, t][:, half * BANK : (half + 1) * BANK],
-                banks[b, t, half][:],
-                ACT.Identity,
-                bias=b1_signed[:, b, t : t + 1],
-                scale=sign[:, b, t : t + 1],
-            )
+        def empty_h(b, t, half, engine="scalar"):
+            dst = h[b, t][:, half * BANK : (half + 1) * BANK]
+            factor, bias = sign[:, b, t : t + 1], b1_signed[:, b, t : t + 1]
+            if engine == "scalar":
+                nc.scalar.activation(dst, banks[b, t, half][:], ACT.Identity, bias=bias, scale=factor)
+            else:
+                nc.vector.tensor_scalar(dst, banks[b, t, half][:], factor, bias, ALU.mult, ALU.add)
 
         x_codes = [tile(f"x_codes{b}", [P, M], U32) for b in range(BLOCKS)]
         x_scales = {1: tile("x_scales1", [P, M], U8)}
@@ -235,21 +244,25 @@ def tile_list_cocoa_supply_tiers_kernel(
 
         def second_product(u, a, first):
             b, ts, entries = UNITS[u]
-            if first:
-                y[u] = psum.tile([P, BANK], F32, name=f"bank{u}")
             count = len(ts)
+            apart = u == 0
+            if first:
+                whole_bank = psum.tile([P, BANK], F32, name=f"bank{u}")
+                y[u] = [whole_bank] * HALVES
+                if apart:
+                    y[u][1] = psum.tile([P, BANK], F32, name=f"bank{len(UNITS) - 1}")
             width = BANK // count
             m0 = entries.start
             for i, t in enumerate(ts):
                 c0 = a * H + b * KP + t * P
                 nc.tensor.matmul_mx(
-                    out=y[u][:, i * width : (i + 1) * width],
+                    out=y[u][i][:, i * width : (i + 1) * width],
                     lhsT=wp_codes[b, t][:, a, :].bitcast(FP4X4),
                     lhsT_scale=wp_sc[:, c0 : c0 + P],
                     rhs=x_codes[a][:, m0 : m0 + width].bitcast(FP8X4),
                     rhs_scale=x_scales[a][:, m0 : m0 + width],
-                    start=first and i == 0,
-                    stop=not first and i == count - 1,
+                    start=first and (apart or i == 0),
+                    stop=not first and (apart or i == count - 1),
                 )
 
         by_half = [(t, half) for half in range(HALVES) for t in range(PACK)]
@@ -258,61 +271,84 @@ def tile_list_cocoa_supply_tiers_kernel(
 
         gather_table(0, (0, 1))
         nc.vector.tensor_copy(v_scales[:], tab_sc[:].indirect(offs_sb[:]))
-        for a in range(PASSES):
+        for a in (1, 2):
             w_bf = tile(f"w_bf0{a}", [P, PACK, P, PACK], BF16, tag=f"w_bf{a}")
             cast_w("scalar", w_bf[:], 0, a, 0)
-            quantize_w(f"0{a}", w_bf, [(0, a, t) for t in range(PACK)])
-        first_product(0, 0, by_half)
-        wp_sc_dealt = tile("wp_sc_dealt", [P, H], U8, tag="w_bf2")
-        nc.vector.tensor_copy(
-            wp_sc_dealt[:].rearrange("p (g t m) -> p g t m", t=PACK, m=P),
-            wp_sc_raw[:].rearrange("p (g m t) -> p g t m", t=PACK, m=P),
+            quantize_w(f"0{a}", w_bf[:], [(0, a, t) for t in range(PACK)])
+        wp_sc_dealt = [tile(f"wp_sc_dealt{a}", [P, H], U8, tag=(AT_DEALT_SC, None)[a]) for a in range(BLOCKS)]
+        for a in range(BLOCKS):
+            nc.vector.tensor_copy(
+                wp_sc_dealt[a][:].rearrange("p (g t m) -> p g t m", t=PACK, m=P),
+                wp_sc_raw[a][:].rearrange("p (g m t) -> p g t m", t=PACK, m=P),
+            )
+
+        def carry_wp_scales(a):
+            for q in range(4):
+                first = 32 * q + 4 * a
+                nc.sync.dma_start(
+                    out=wp_sc[32 * q : 32 * q + 4, a * H : (a + 1) * H].bitcast(I32),
+                    in_=wp_sc_dealt[a][first : 32 * q + 32 : 8, :].bitcast(I32),
+                )
+
+        carry_wp_scales(0)
+        nc.sync.dma_start(
+            out=wp_raw[:].bitcast(I32).rearrange("p (a c) -> p a c", a=BLOCKS),
+            in_=wp_words.bitcast(I32).rearrange("a p c -> p a c"),
         )
+        nc.sync.dma_start(pos2_sb[:], pos2)
+        carry_wp_scales(1)
         for half in range(HALVES):
             gather_table(1, (half,))
         first_product(0, 1, by_half)
         gather_table(2, (0,))
         gather_table(2, (1,))
-        first_product(0, 2, opening)
+        first_product(0, 2, by_half[:PACK])
+        w_bf00 = tile("w_bf00", [P, 2, P, PACK], BF16, tag="w_bf1")
+        w_bf00b = tile("w_bf00b", [P, 2, P, PACK], BF16, tag="w_bf2")
+        cast_w("vector", w_bf00[:], 0, 0, 0, slice(0, FIRST_COLS))
+        cast_w("scalar", w_bf00[:], 0, 0, 0, slice(FIRST_COLS, P))
+        cast_w("vector", w_bf00b[:], 0, 0, 2, slice(0, SECOND_COLS))
+        cast_w("scalar", w_bf00b[:], 0, 0, 2, slice(SECOND_COLS, P))
+        quantize_w("00", w_bf00[:], [(0, 0, 0), (0, 0, 1)])
+        quantize_w("00b", w_bf00b[:], [(0, 0, 2), (0, 0, 3)])
         for t, half in opening:
-            empty_h(0, t, half)
+            first_product(0, 0, [(t, half)])
+            if half == 1:
+                first_product(0, 2, [(t, half)])
+        for t, half in opening:
+            empty_h(0, t, half, "vector" if (t, half) == (0, 0) else "scalar")
 
-        w_bf10 = tile("w_bf10", [P, PACK, P, PACK], BF16, tag="w_bf0")
-        cast_w("vector", w_bf10[:], 1, 0, 0)
-        quantize_w("10", w_bf10, [(1, 0, t) for t in range(PACK)])
+        shift = RAW - PACK * 32
+        joined = tile("joined", [P, 2 * shift + RAW // 2], BF16)
+        w_bf10 = joined[:, :RAW].rearrange("p (t m j) -> p t m j", t=PACK, j=PACK)
+        w_bf11 = joined[:, shift : shift + RAW].rearrange("p (t m j) -> p t m j", t=PACK, j=PACK)
+        w_bf12b = joined[:, 2 * shift :].rearrange("p (t m j) -> p t m j", t=2, j=PACK)
+        for first in (0, 2):
+            cast_w("vector", w_bf10[:, first : first + 2], 1, 0, first)
+        for first in (0, 2):
+            quantize_w(f"10{first}", w_bf10[:, first : first + 2], [(1, 0, first), (1, 0, first + 1)])
         first_product(1, 0, opening)
-        pairs = tile("pairs", [P, (4 * P - GPSIMD_COLS) * PACK], BF16, tag=14272)
-        w_bf11 = pairs[:, : 2 * P * PACK].rearrange("p (t m j) -> p t m j", t=2, j=PACK)
-        w_bf11b = pairs[:, (2 * P - GPSIMD_COLS) * PACK :].rearrange("p (t m j) -> p t m j", t=2, j=PACK)
-        cast_w("vector", w_bf11, 1, 1, 0)
-        cast_w("vector", w_bf11b, 1, 1, 2, slice(GPSIMD_COLS, P))
-        quantize_w("11", w_bf11, [(1, 1, 0), (1, 1, 1)])
-        cast_w("gpsimd", w_bf11b, 1, 1, 2, slice(0, GPSIMD_COLS))
-        up_first = tile("up_first", [P, PACK, HALF_M], F32)
-        for t in range(PACK):
+        cast_w("gpsimd", w_bf11, 1, 1, 0, slice(0, GPSIMD_COLS))
+        cast_w("scalar", w_bf11, 1, 1, 0, slice(GPSIMD_COLS, P))
+        for t in range(PACK - 1):
             gather_up(up_first[:, t, :], 0, t, 0, HALF_M)
-        w_bf12 = tile("w_bf12", [P, 2, P, PACK], BF16, tag=10240)
-        cast_w("scalar", w_bf12[:], 1, 2, 0)
-        quantize_w("12", w_bf12, [(1, 2, 0), (1, 2, 1)])
-        quantize_w("11b", w_bf11b, [(1, 1, 2), (1, 1, 3)], 10304)
-        w_bf12b = tile("w_bf12b", [P, 2, P, PACK], BF16, tag=14272)
-        cast_w("gpsimd", w_bf12b[:], 1, 2, 2)
-        x_first = tile("x_first", [P, HALF_M, PACK], BF16, tag=12224)
-        round_x(x_first[:], up_first[:])
-        up_second = tile("up_second", [P, PACK, HALF_M], F32, tag=6208)
-        for t in range(PACK):
+        gather_up(up_second[:, 0, :], 0, 0, HALF_M, HALF_M)
+        gather_up(up_first[:, PACK - 1, :], 0, PACK - 1, 0, HALF_M)
+        cast_w("scalar", w_bf12, 1, 2, 0, slice(P - SCALAR_COLS, P))
+        x_first = tile("x_first", [P, HALF_M, PACK], BF16, tag=AT_DEALT_SC - 1984)
+        round_x(x_first[:], up_first)
+        cast_w("vector", w_bf12, 1, 2, 0, slice(0, P - SCALAR_COLS))
+        cast_w("vector", w_bf12b, 1, 2, 2, slice(GPSIMD_LAST_COLS, P))
+        quantize_w("11", w_bf11[:, :2], [(1, 1, 0), (1, 1, 1)], None, AT_DEALT_SC + 64)
+        quantize_w("12", w_bf12, [(1, 2, 0), (1, 2, 1)], None, AT_DEALT_SC + 320)
+        quantize_w("11b", w_bf11[:, 2:], [(1, 1, 2), (1, 1, 3)], None, AT_DEALT_SC + 576)
+        cast_w("gpsimd", w_bf12b, 1, 2, 2, slice(0, GPSIMD_LAST_COLS))
+        for t in range(1, PACK):
             gather_up(up_second[:, t, :], 0, t, HALF_M, HALF_M)
         quantize_w("12b", w_bf12b, [(1, 2, 2), (1, 2, 3)])
         for bank in by_slice:
             for a in (1, 2):
                 first_product(1, a, [bank])
-        for a in range(BLOCKS):
-            for q in range(4):
-                first = 4 * (16 * a + 4 * q)
-                nc.sync.dma_start(
-                    out=wp_sc[32 * q : 32 * q + 4, a * H : (a + 1) * H].bitcast(I32),
-                    in_=wp_sc_dealt[first : first + 16 : 4, :].bitcast(I32),
-                )
         up_last = tile("up_last", [P, PACK, M], F32, tag=AT_UP_LAST)
         for t in range(PACK):
             for half in range(HALVES):
@@ -324,7 +360,7 @@ def tile_list_cocoa_supply_tiers_kernel(
         second_product(0, 0, True)
         gather_up(up_last[:, PACK - 1, HALF_M:], 1, PACK - 1, HALF_M, HALF_M)
         x_second = tile("x_second", [P, HALF_M, PACK], BF16, tag="w_codes12b")
-        round_x(x_second[:], up_second[:])
+        round_x(x_second[:], up_second)
         quantize_x(0, HALF_M, x_second[:])
         second_product(1, 0, True)
         x_third = tile("x_third", [P, HALF_M, PACK], BF16)
@@ -340,8 +376,8 @@ def tile_list_cocoa_supply_tiers_kernel(
         for u in range(2, len(UNITS)):
             second_product(u, 1, True)
             second_product(u, 0, False)
-        down = tile("down", [P, M], F32, tag=AT_UP_LAST + 2048)
-        nc.vector.tensor_copy(down[:], h[SLICES[-1]][:].indirect(pos2_sb[:]))
+        down = tile("down", [P, HALF_M], F32, tag=AT_UP_LAST + 2048)
+        nc.vector.tensor_copy(down[:], h[SLICES[-1]][:].indirect(pos2_sb[:, HALF_M // 16 :]))
 
         n = len(UNITS)
         whole = slice(0, M)
@@ -358,7 +394,7 @@ def tile_list_cocoa_supply_tiers_kernel(
         def magnitude(u, cols=whole):
             if u not in mag:
                 mag[u] = tile(f"mag{u}", [P, M], F32, tag=AT_MAG + 2048 if u == 2 else None)
-            nc.scalar.activation(mag[u][:, cols], y[u][:, cols], ACT.Abs)
+            nc.scalar.activation(mag[u][:, cols], y[u][cols.start // HALF_M][:, cols], ACT.Abs)
 
         def root(u, cols=whole):
             nc.scalar.activation(roots[:, u, cols], mag[u][:, cols], ACT.Abs_reciprocal_sqrt, bias=1.0)
@@ -381,7 +417,11 @@ def tile_list_cocoa_supply_tiers_kernel(
             else:
                 res = results[:, u, :]
             if u == n - 1:
-                nc.vector.tensor_tensor(res[:, cols], damp[:, u, cols], down[:, cols], ALU.mult)
+                if cols.start == 0:
+                    picked = h[b, ts[0]][:].indirect(pos2_sb[:, : HALF_M // 16])
+                    nc.vector.tensor_tensor(res[:, cols], picked, damp[:, u, cols], ALU.mult)
+                else:
+                    nc.vector.tensor_tensor(res[:, cols], damp[:, u, cols], down[:], ALU.mult)
                 nc.sync.dma_start(out=out_rows[:, ts[0], cols], in_=res[:, cols])
                 return
             offsets = pos2_sb[:, entries.start // 16 : entries.stop // 16]
@@ -391,8 +431,10 @@ def tile_list_cocoa_supply_tiers_kernel(
                 out=out_rows[:, ts[0] : ts[-1] + 1, entries], in_=res.rearrange("p (t m) -> p t m", t=len(ts))
             )
 
-        magnitude(0)
-        root(0)
+        for cols in halves:
+            magnitude(0, cols)
+        for cols in halves:
+            root(0, cols)
         square(0)
         finish(0)
         for u in (1, 3):

@@ -100,8 +100,8 @@ def tile_list_cocoa_supply_tiers_kernel(
                 in_=w1[a * KP : (a + 1) * KP, b * KP : (b + 1) * KP].rearrange("(p j) c -> p j c", j=PACK),
             )
 
-        nc.sync.dma_start(offs_sb[:], offs)
         load_table(0)
+        nc.sync.dma_start(offs_sb[:], offs)
         for q in range(4):
             nc.gpsimd.dma_start(
                 out=tab_sc[32 * q + 4 : 32 * q + 4 + 4 * PASSES, :].bitcast(I32),

from contextlib import ExitStack

import concourse.mybir as mybir

K, H, T, S, M = 1536, 1024, 4096, 1024, 512
FLOPS = 2 * K * H * S + 2 * H * H * M

F32 = mybir.dt.float32
BF16 = mybir.dt.bfloat16
I32 = mybir.dt.int32
U32 = mybir.dt.uint32
U16 = mybir.dt.uint16
U8 = mybir.dt.uint8
FP8X4 = mybir.dt.float8_e4m3fn_x4
FP4X4 = mybir.dt.float4_e2m1fn_x4
ACT = mybir.ActivationFunctionType
ALU = mybir.AluOpType

P = 128
PACK = 4
KP = P * PACK
BANK = 512
PASSES = K // KP
BLOCKS = H // KP
HALVES = S // BANK
HALF_M = M // 2
SLICES = [(b, t) for b in range(BLOCKS) for t in range(PACK)]
UNITS = [(0, (0, 1), slice(m0, m0 + HALF_M)) for m0 in (0, HALF_M)]
UNITS = UNITS + [(b, (t,), slice(0, M)) for b, t in SLICES[4:7] + SLICES[2:4] + SLICES[7:]]
SMALLEST_NORMAL = 2.0**-126
SQUARED_ON_VECTOR = 3
GPSIMD_COLS = 60
FIRST_COLS = 80
SECOND_COLS = 48
SCALAR_COLS = 72
GPSIMD_LAST_COLS = 64
RAW = PACK * KP

AT_TAB_SC = 0
AT_WP_SC = 4096
AT_WP_WORDS = 6144
AT_DEALT_SC = 12224
AT_SIGN = 13248
AT_BIAS = 14272
AT_UP_LAST = 14784
AT_MAG = 22976


def tile_list_cocoa_supply_tiers_kernel(
    tc, tab_words, tab_scales, offs, pos1, pos2, w1, b1, wp_words, wp_scales, gd, out
):
    nc = tc.nc
    with ExitStack() as ctx:
        lists = ctx.enter_context(tc.tile_pool(name="lists", bufs=1))
        keep = ctx.enter_context(tc.tile_pool(name="keep", bufs=1))
        shared = ctx.enter_context(tc.tile_pool(name="shared", bufs=1))
        psum = ctx.enter_context(tc.psum_pool(name="psum", bufs=1))

        def tile(name, shape, dtype, tag=None):
            if isinstance(tag, int):
                return shared.tile(shape, dtype, name=name, offset=tag, align_bytes=64)
            return keep.tile(shape, dtype, name=name, tag=tag or name, align_bytes=64)

        offs_sb = lists.tile([P, S // 16], U16, name="offs_sb")
        pos1_sb = lists.tile([P, M // 16], U16, name="pos1_sb")
        pos2_sb = lists.tile([P, M // 16], U16, name="pos2_sb")

        tab_sc = tile("tab_sc", [P, T], U8, tag=AT_TAB_SC)
        wp_sc_raw = [tile(f"wp_sc_raw{a}", [P, H], U8, tag=(AT_WP_SC, AT_WP_WORDS)[a]) for a in range(BLOCKS)]
        wp_sc = tile("wp_sc", [P, BLOCKS * H], U8)
        nc.vector.memset(tab_sc[:].bitcast(I32), 0)
        for a in range(BLOCKS):
            nc.vector.memset(wp_sc_raw[a][:].bitcast(I32), 0)
        nc.vector.memset(wp_sc[:].bitcast(I32), 0)
        rows = tile("rows", [P, P], F32)
        nc.vector.memset(rows[:], 0.0)
        tab_w = [tile(f"tab_w{a}", [P, T], U32) for a in range(PASSES)]
        stage = tile("stage", [P, RAW + (PACK - 1) * HALF_M], F32)
        w_raw = {
            (b, a): tile(f"w_raw{b}{a}", [P, RAW], F32)[:]
            for b in range(BLOCKS)
            for a in range(PASSES)
            if (b, a) != (1, 0)
        }
        w_raw[1, 0] = stage[:, :RAW]
        up_first = stage[:, : PACK * HALF_M].rearrange("p (t m) -> p t m", t=PACK)
        up_second = stage[:, RAW - HALF_M :].rearrange("p (t m) -> p t m", t=PACK)
        w_bf12 = stage[:, RAW + P : RAW + P + KP].bitcast(BF16).rearrange("p (t m j) -> p t m j", t=2, j=PACK)
        wp_raw = tile("wp_raw", [P, BLOCKS * 2 * H], U8, tag=AT_WP_WORDS)

        def load_table(a):
            nc.sync.dma_start(
                out=tab_w[a][:].bitcast(I32),
                in_=tab_words[a].rearrange("p c i -> p (c i)").bitcast(I32),
            )

        def load_w(b, a):
            nc.sync.dma_start(
                out=w_raw[b, a].rearrange("p (j c) -> p j c", j=PACK),
                in_=w1[a * KP : (a + 1) * KP, b * KP : (b + 1) * KP].rearrange("(p j) c -> p j c", j=PACK),
            )

        load_table(0)
        nc.sync.dma_start(offs_sb[:], offs)
        for q in range(4):
            nc.gpsimd.dma_start(
                out=tab_sc[32 * q + 4 : 32 * q + 4 + 4 * PASSES, :].bitcast(I32),
                in_=tab_scales[:, 4 * q : 4 * q + 4, :].bitcast(I32),
            )
        nc.scalar.dma_start(out=rows[1:P:16, :], in_=gd.rearrange("(b q c) -> q b c", b=BLOCKS, c=P))
        load_w(0, 1)
        load_w(0, 2)
        nc.scalar.dma_start(out=rows[0:P:16, :], in_=b1.rearrange("(b q c) -> q b c", b=BLOCKS, c=P))
        for a in range(BLOCKS):
            nc.gpsimd.dma_start(out=wp_sc_raw[a][4 * a : P : 8, :].bitcast(I32), in_=wp_scales[a].bitcast(I32))
        load_table(1)
        load_table(2)
        load_w(0, 0)
        load_w(1, 0)
        nc.sync.dma_start(pos1_sb[:], pos1)
        load_w(1, 1)
        load_w(1, 2)

        dealt_rows = tile("dealt_rows", [P, PACK, 32], F32)
        columns = tile("columns", [P, PACK, BLOCKS, 16], F32)
        nc.vector.tensor_copy(dealt_rows[:], rows[:].rearrange("p (j t) -> p t j", t=PACK))
        nc.vector.transpose(
            columns[:].rearrange("p t b i -> p (t b i)"), dealt_rows[:].rearrange("p t j -> p (t j)")
        )
        b1_sb = columns[:, :, :, 0].rearrange("p t b -> p b t")
        gd_sb = columns[:, :, :, 1].rearrange("p t b -> p b t")
        gd_abs = tile("gd_abs", [P, BLOCKS, PACK], F32)
        gd_floor = tile("gd_floor", [P, BLOCKS, PACK], F32)
        gd_rsqrt = tile("gd_rsqrt", [P, BLOCKS, PACK], F32)
        gd_root = tile("gd_root", [P, BLOCKS, PACK], F32)
        positive = tile("positive", [P, BLOCKS, PACK], F32)
        sign = tile("sign", [P, BLOCKS, PACK], F32, tag=AT_SIGN)
        b1_signed = tile("b1_signed", [P, BLOCKS, PACK], F32, tag=AT_BIAS)
        nc.vector.tensor_scalar(positive[:], gd_sb, 0.0, None, ALU.is_ge)
        nc.vector.tensor_scalar(sign[:], positive[:], 2.0, -1.0, ALU.mult, ALU.add)
        nc.vector.tensor_tensor(gd_abs[:], gd_sb, sign[:], ALU.mult)
        nc.vector.tensor_tensor(b1_signed[:], b1_sb, sign[:], ALU.mult)
        nc.vector.tensor_scalar(gd_floor[:], gd_abs[:], SMALLEST_NORMAL, None, ALU.max)
        nc.scalar.activation(gd_rsqrt[:], gd_floor[:], ACT.Abs_reciprocal_sqrt)
        nc.vector.tensor_tensor(gd_root[:], gd_abs[:], gd_rsqrt[:], ALU.mult)

        v_codes = {}
        v_scales = tile("v_scales", [P, S], U8)
        w_codes = {}
        w_scales = {}

        def gather_table(a, halves):
            first, count = halves[0], len(halves)
            place = (AT_TAB_SC, AT_WP_SC)[first] if a == 1 else None
            picked = tile(f"v_codes{a}{first}", [P, count * BANK], U32, tag=place)
            nc.vector.tensor_copy(
                picked[:], tab_w[a][:].indirect(offs_sb[:, first * BANK // 16 : (first + count) * BANK // 16])
            )
            for i, half in enumerate(halves):
                v_codes[a, half] = picked[:, i * BANK : (i + 1) * BANK]

        def cast_w(engine, w_bf, b, a, first, cols=slice(0, P)):
            count = w_bf.shape[1]
            dst = w_bf.rearrange("p t m j -> p m j t")[:, cols]
            src = w_raw[b, a].rearrange("p (j m t) -> p m j t", j=PACK, t=PACK)[:, cols, :, first : first + count]
            if engine == "scalar":
                nc.scalar.activation(dst, src, ACT.Copy)
            elif engine == "vector":
                nc.vector.tensor_copy(dst, src)
            else:
                dst = dst.rearrange("p m j t -> p m t j")
                src = src.rearrange("p m j t -> p m t j")
                nc.gpsimd.tensor_scalar(dst, src, 1.0, 0.0, ALU.mult, ALU.add)

        def quantize_w(name, w_bf, keys, tag=None, scale_tag=None):
            codes = tile(f"w_codes{name}", [P, len(keys) * P], U32, tag=tag)
            scales = tile(f"w_scales{name}", [P, len(keys) * P], U8, tag=scale_tag)
            nc.vector.quantize_mx(
                out=codes[:].bitcast(FP8X4), scales=scales[:], in_=w_bf.rearrange("p t m j -> p (t m j)")
            )
            for i, key in enumerate(keys):
                w_codes[key] = codes[:, i * P : (i + 1) * P]
                w_scales[key] = scales[:, i * P : (i + 1) * P]

        banks = {}

        def first_product(b, a, order):
            for t, half in order:
                passes = (0, 1, 2) if b == 1 else ((1, 2, 0), (1, 0, 2))[half]
                if a == passes[0]:
                    banks[b, t, half] = psum.tile([P, BANK], F32, name=f"bank{HALVES * t + half}")
                nc.tensor.matmul_mx(
                    out=banks[b, t, half][:],
                    lhsT=w_codes[b, a, t].bitcast(FP8X4),
                    lhsT_scale=w_scales[b, a, t],
                    rhs=v_codes[a, half].bitcast(FP8X4),
                    rhs_scale=v_scales[4 * (a + 1) : P, half * BANK : (half + 1) * BANK],
                    start=(a == passes[0]),
                    stop=(a == passes[-1]),
                )

        h = {(b, t): tile(f"h{b}{t}", [P, S], F32) for b, t in SLICES}

        def empty_h(b, t, half, engine="scalar"):
            dst = h[b, t][:, half * BANK : (half + 1) * BANK]
            factor, bias = sign[:, b, t : t + 1], b1_signed[:, b, t : t + 1]
            if engine == "scalar":
                nc.scalar.activation(dst, banks[b, t, half][:], ACT.Identity, bias=bias, scale=factor)
            else:
                nc.vector.tensor_scalar(dst, banks[b, t, half][:], factor, bias, ALU.mult, ALU.add)

        x_codes = [tile(f"x_codes{b}", [P, M], U32) for b in range(BLOCKS)]
        x_scales = {1: tile("x_scales1", [P, M], U8)}

        def gather_up(dst, b, t, m0, width):
            nc.vector.tensor_copy(dst, h[b, t][:].indirect(pos1_sb[:, m0 // 16 : (m0 + width) // 16]))

        def round_x(x_bf, up):
            nc.scalar.activation(
                x_bf.rearrange("p (c i) t -> p c t i", i=2),
                up.rearrange("p t (c i) -> p c t i", i=2),
                ACT.Abs,
            )

        def quantize_x(b, m0, x_bf):
            nc.vector.quantize_mx(
                out=x_codes[b][:, m0 : m0 + HALF_M].bitcast(FP8X4),
                scales=x_scales[b][:, m0 : m0 + HALF_M],
                in_=x_bf.rearrange("p m t -> p (m t)"),
            )

        wp_codes = {}

        def deal_wp_words(b, first, count, tag):
            dealt = tile(f"wp_codes{b}{first}", [P, BLOCKS, count * 2 * P], U8, tag=tag)
            words = wp_raw[:].bitcast(U16).rearrange("p (a b m t) -> p b a t m", a=BLOCKS, b=BLOCKS, t=PACK)
            nc.vector.tensor_copy(
                dealt[:].bitcast(U16).rearrange("p a (t m) -> p a t m", t=count), words[:, b, :, first : first + count]
            )
            for i in range(count):
                wp_codes[b, first + i] = dealt[:, :, i * 2 * P : (i + 1) * 2 * P]

        y = {}

        def second_product(u, a, first):
            b, ts, entries = UNITS[u]
            count = len(ts)
            apart = u == 0
            if first:
                whole_bank = psum.tile([P, BANK], F32, name=f"bank{u}")
                y[u] = [whole_bank] * HALVES
                if apart:
                    y[u][1] = psum.tile([P, BANK], F32, name=f"bank{len(UNITS) - 1}")
            width = BANK // count
            m0 = entries.start
            for i, t in enumerate(ts):
                c0 = a * H + b * KP + t * P
                nc.tensor.matmul_mx(
                    out=y[u][i][:, i * width : (i + 1) * width],
                    lhsT=wp_codes[b, t][:, a, :].bitcast(FP4X4),
                    lhsT_scale=wp_sc[:, c0 : c0 + P],
                    rhs=x_codes[a][:, m0 : m0 + width].bitcast(FP8X4),
                    rhs_scale=x_scales[a][:, m0 : m0 + width],
                    start=first and (apart or i == 0),
                    stop=not first and (apart or i == count - 1),
                )

        by_half = [(t, half) for half in range(HALVES) for t in range(PACK)]
        by_slice = [(t, half) for t in range(PACK) for half in range(HALVES)]
        opening = [(0, 0), (1, 0), (0, 1), (1, 1)] + by_slice[4:]

        gather_table(0, (0, 1))
        nc.vector.tensor_copy(v_scales[:], tab_sc[:].indirect(offs_sb[:]))
        for a in (1, 2):
            w_bf = tile(f"w_bf0{a}", [P, PACK, P, PACK], BF16, tag=f"w_bf{a}")
            cast_w("scalar", w_bf[:], 0, a, 0)
            quantize_w(f"0{a}", w_bf[:], [(0, a, t) for t in range(PACK)])
        wp_sc_dealt = [tile(f"wp_sc_dealt{a}", [P, H], U8, tag=(AT_DEALT_SC, None)[a]) for a in range(BLOCKS)]
        for a in range(BLOCKS):
            nc.vector.tensor_copy(
                wp_sc_dealt[a][:].rearrange("p (g t m) -> p g t m", t=PACK, m=P),
                wp_sc_raw[a][:].rearrange("p (g m t) -> p g t m", t=PACK, m=P),
            )

        def carry_wp_scales(a):
            for q in range(4):
                first = 32 * q + 4 * a
                nc.sync.dma_start(
                    out=wp_sc[32 * q : 32 * q + 4, a * H : (a + 1) * H].bitcast(I32),
                    in_=wp_sc_dealt[a][first : 32 * q + 32 : 8, :].bitcast(I32),
                )

        carry_wp_scales(0)
        nc.sync.dma_start(
            out=wp_raw[:].bitcast(I32).rearrange("p (a c) -> p a c", a=BLOCKS),
            in_=wp_words.bitcast(I32).rearrange("a p c -> p a c"),
        )
        nc.sync.dma_start(pos2_sb[:], pos2)
        carry_wp_scales(1)
        for half in range(HALVES):
            gather_table(1, (half,))
        first_product(0, 1, by_half)
        gather_table(2, (0,))
        gather_table(2, (1,))
        first_product(0, 2, by_half[:PACK])
        w_bf00 = tile("w_bf00", [P, 2, P, PACK], BF16, tag="w_bf1")
        w_bf00b = tile("w_bf00b", [P, 2, P, PACK], BF16, tag="w_bf2")
        cast_w("vector", w_bf00[:], 0, 0, 0, slice(0, FIRST_COLS))
        cast_w("scalar", w_bf00[:], 0, 0, 0, slice(FIRST_COLS, P))
        cast_w("vector", w_bf00b[:], 0, 0, 2, slice(0, SECOND_COLS))
        cast_w("scalar", w_bf00b[:], 0, 0, 2, slice(SECOND_COLS, P))
        quantize_w("00", w_bf00[:], [(0, 0, 0), (0, 0, 1)])
        quantize_w("00b", w_bf00b[:], [(0, 0, 2), (0, 0, 3)])
        for t, half in opening:
            first_product(0, 0, [(t, half)])
            if half == 1:
                first_product(0, 2, [(t, half)])
        for t, half in opening:
            empty_h(0, t, half, "vector" if (t, half) == (0, 0) else "scalar")

        shift = RAW - PACK * 32
        joined = tile("joined", [P, 2 * shift + RAW // 2], BF16)
        w_bf10 = joined[:, :RAW].rearrange("p (t m j) -> p t m j", t=PACK, j=PACK)
        w_bf11 = joined[:, shift : shift + RAW].rearrange("p (t m j) -> p t m j", t=PACK, j=PACK)
        w_bf12b = joined[:, 2 * shift :].rearrange("p (t m j) -> p t m j", t=2, j=PACK)
        for first in (0, 2):
            cast_w("vector", w_bf10[:, first : first + 2], 1, 0, first)
        for first in (0, 2):
            quantize_w(f"10{first}", w_bf10[:, first : first + 2], [(1, 0, first), (1, 0, first + 1)])
        first_product(1, 0, opening)
        cast_w("gpsimd", w_bf11, 1, 1, 0, slice(0, GPSIMD_COLS))
        cast_w("scalar", w_bf11, 1, 1, 0, slice(GPSIMD_COLS, P))
        for t in range(PACK - 1):
            gather_up(up_first[:, t, :], 0, t, 0, HALF_M)
        gather_up(up_second[:, 0, :], 0, 0, HALF_M, HALF_M)
        gather_up(up_first[:, PACK - 1, :], 0, PACK - 1, 0, HALF_M)
        cast_w("scalar", w_bf12, 1, 2, 0, slice(P - SCALAR_COLS, P))
        x_first = tile("x_first", [P, HALF_M, PACK], BF16, tag=AT_DEALT_SC - 1984)
        round_x(x_first[:], up_first)
        cast_w("vector", w_bf12, 1, 2, 0, slice(0, P - SCALAR_COLS))
        cast_w("vector", w_bf12b, 1, 2, 2, slice(GPSIMD_LAST_COLS, P))
        quantize_w("11", w_bf11[:, :2], [(1, 1, 0), (1, 1, 1)], None, AT_DEALT_SC + 64)
        quantize_w("12", w_bf12, [(1, 2, 0), (1, 2, 1)], None, AT_DEALT_SC + 320)
        quantize_w("11b", w_bf11[:, 2:], [(1, 1, 2), (1, 1, 3)], None, AT_DEALT_SC + 576)
        cast_w("gpsimd", w_bf12b, 1, 2, 2, slice(0, GPSIMD_LAST_COLS))
        for t in range(1, PACK):
            gather_up(up_second[:, t, :], 0, t, HALF_M, HALF_M)
        quantize_w("12b", w_bf12b, [(1, 2, 2), (1, 2, 3)])
        for bank in by_slice:
            for a in (1, 2):
                first_product(1, a, [bank])
        up_last = tile("up_last", [P, PACK, M], F32, tag=AT_UP_LAST)
        for t in range(PACK):
            for half in range(HALVES):
                empty_h(1, t, half)
            gather_up(up_last[:, t, : M if t < PACK - 1 else HALF_M], 1, t, 0, M if t < PACK - 1 else HALF_M)
        deal_wp_words(0, 0, 2, AT_SIGN)
        x_scales[0] = tile("x_scales0", [P, M], U8, tag=AT_BIAS)
        quantize_x(0, 0, x_first[:])
        second_product(0, 0, True)
        gather_up(up_last[:, PACK - 1, HALF_M:], 1, PACK - 1, HALF_M, HALF_M)
        x_second = tile("x_second", [P, HALF_M, PACK], BF16, tag="w_codes12b")
        round_x(x_second[:], up_second)
        quantize_x(0, HALF_M, x_second[:])
        second_product(1, 0, True)
        x_third = tile("x_third", [P, HALF_M, PACK], BF16)
        round_x(x_third[:], up_last[:, :, :HALF_M])
        quantize_x(1, 0, x_third[:])
        second_product(0, 1, False)
        deal_wp_words(1, 0, PACK, "x_third")
        x_fourth = tile("x_fourth", [P, HALF_M, PACK], BF16)
        round_x(x_fourth[:], up_last[:, :, HALF_M:])
        quantize_x(1, HALF_M, x_fourth[:])
        second_product(1, 1, False)
        deal_wp_words(0, 2, 2, AT_UP_LAST)
        for u in range(2, len(UNITS)):
            second_product(u, 1, True)
            second_product(u, 0, False)
        down = tile("down", [P, HALF_M], F32, tag=AT_UP_LAST + 2048)
        nc.vector.tensor_copy(down[:], h[SLICES[-1]][:].indirect(pos2_sb[:, HALF_M // 16 :]))

        n = len(UNITS)
        whole = slice(0, M)
        halves = [slice(0, HALF_M), slice(HALF_M, M)]
        mag = {}
        roots = tile("roots", [P, n, M], F32, tag="tab_w0")
        damp = tile("damp", [P, n, M], F32, tag="tab_w1")
        results = tile("results", [P, n, M], F32, tag="tab_w2")

        def runs(u, cols):
            ts = UNITS[u][1]
            return [(ts[0], cols)] if len(ts) == 1 else list(zip(ts, halves))

        def magnitude(u, cols=whole):
            if u not in mag:
                mag[u] = tile(f"mag{u}", [P, M], F32, tag=AT_MAG + 2048 if u == 2 else None)
            nc.scalar.activation(mag[u][:, cols], y[u][cols.start // HALF_M][:, cols], ACT.Abs)

        def root(u, cols=whole):
            nc.scalar.activation(roots[:, u, cols], mag[u][:, cols], ACT.Abs_reciprocal_sqrt, bias=1.0)

        def square(u, cols=whole):
            b = UNITS[u][0]
            for t, run in runs(u, cols):
                if u < SQUARED_ON_VECTOR:
                    nc.vector.scalar_tensor_tensor(
                        damp[:, u, run], roots[:, u, run], gd_abs[:, b, t : t + 1], roots[:, u, run], ALU.mult, ALU.mult
                    )
                else:
                    nc.scalar.activation(damp[:, u, run], roots[:, u, run], ACT.Square, scale=gd_root[:, b, t : t + 1])

        def finish(u, cols=whole):
            b, ts, entries = UNITS[u]
            out_rows = out[b * KP : (b + 1) * KP, :].rearrange("(p t) m -> p t m", t=PACK)
            if 1 <= u < SQUARED_ON_VECTOR - 1:
                res = tile(f"res{u}", [P, M], F32, tag=AT_MAG + 2048 if u == 1 else f"mag{u + 1}")[:]
            else:
                res = results[:, u, :]
            if u == n - 1:
                if cols.start == 0:
                    picked = h[b, ts[0]][:].indirect(pos2_sb[:, : HALF_M // 16])
                    nc.vector.tensor_tensor(res[:, cols], picked, damp[:, u, cols], ALU.mult)
                else:
                    nc.vector.tensor_tensor(res[:, cols], damp[:, u, cols], down[:], ALU.mult)
                nc.sync.dma_start(out=out_rows[:, ts[0], cols], in_=res[:, cols])
                return
            offsets = pos2_sb[:, entries.start // 16 : entries.stop // 16]
            for t, run in runs(u, cols):
                nc.vector.tensor_tensor(res[:, run], h[b, t][:].indirect(offsets), damp[:, u, run], ALU.mult)
            nc.sync.dma_start(
                out=out_rows[:, ts[0] : ts[-1] + 1, entries], in_=res.rearrange("p (t m) -> p t m", t=len(ts))
            )

        for cols in halves:
            magnitude(0, cols)
        for cols in halves:
            root(0, cols)
        square(0)
        finish(0)
        for u in (1, 3):
            magnitude(u)
            magnitude(u + 1)
            root(u)
            root(u + 1)
            if u == 1:
                square(1)
                square(2)
                finish(1)
        finish(2)
        square(3)
        finish(3)
        for u in range(4, n - 1):
            magnitude(u + 1, whole if u + 1 < n - 1 else halves[0])
            square(u)
            finish(u)
            if u + 1 < n - 1:
                root(u + 1)
        magnitude(n - 1, halves[1])
        for cols in halves:
            root(n - 1, cols)
        for cols in halves:
            square(n - 1, cols)
            finish(n - 1, cols)
